import numpy as np
import ml_dtypes


def mxq(x, axis, fmt="e4m3"):
    dtype, down = {"e4m3": (ml_dtypes.float8_e4m3fn, 7), "e5m2": (ml_dtypes.float8_e5m2, 14)}[fmt]
    v = np.moveaxis(np.asarray(x, np.float32).astype(ml_dtypes.bfloat16).astype(np.float64), axis, -1)
    blocks = v.reshape(v.shape[:-1] + (-1, 32))
    amax = np.abs(blocks).max(-1, keepdims=True)
    byte = np.maximum(np.where(amax > 0, np.frexp(amax)[1] - 1 + 127, 0) - down, 1)
    scale = np.exp2(byte - 127.0)
    codes = (blocks / scale).astype(np.float32).astype(dtype).astype(np.float64)
    return np.moveaxis((codes * scale).reshape(v.shape), -1, axis)


WIDE = False


def mx_kscale(k):
    if not WIDE:
        return np.ones(k)
    levels = np.array([10, -10, 5, -5, 0])
    if k % 512:
        return np.exp2(np.random.permutation(np.resize(levels, k // 32))).repeat(32)
    a = np.empty((k // 512, 16))
    for p in range(k // 512):
        a[p, :8] = np.random.permutation(np.resize(levels, 8))
        for g in range(8):
            far = levels[np.abs(levels - a[p, g]) >= 10]
            a[p, g + 8] = far[np.random.randint(len(far))]
    return np.exp2(a.ravel()).repeat(32)


BF16 = ml_dtypes.bfloat16


def bf(x):
    return np.asarray(x, np.float32).astype(BF16)


def f64(x):
    return np.asarray(x).astype(np.float64)


E2M1 = np.array([0.0, 0.5, 1.0, 1.5, 2.0, 3.0, 4.0, 6.0, -0.0, -0.5, -1.0, -1.5, -2.0, -3.0, -4.0, -6.0])


def pack_weight(w, fmt):
    k, n = w.shape
    w = f64(bf(w)).reshape(k // 32, 32, n)
    amax = np.abs(w).max(1)
    if fmt == "e4m3":
        byte = np.frexp(amax)[1] - 1 + 127 - 7
    else:
        mant, ex = np.frexp(amax / 6.0)
        byte = np.where(mant > 0.5, ex, ex - 1) + 127
    byte = np.clip(np.where(amax > 0, byte, 1), 1, 254)
    scaled = (w * np.exp2(127.0 - byte)[:, None, :]).reshape(k, n).astype(np.float32)
    by_word = np.ascontiguousarray(scaled.reshape(k // 512, 128, 4, n).transpose(0, 1, 3, 2))
    if fmt == "e4m3":
        words = by_word.astype(ml_dtypes.float8_e4m3fn).view(np.uint8)
    else:
        c = by_word.astype(ml_dtypes.float4_e2m1fn).view(np.uint8) & 0xF
        words = c[..., 0::2] | (c[..., 1::2] << 4)
    return np.ascontiguousarray(words), np.ascontiguousarray(byte.astype(np.uint8).reshape(k // 512, 16, n))


def unpack_weight(words, scales, fmt):
    g, p, n, _ = words.shape
    if fmt == "e4m3":
        vals = np.ascontiguousarray(words).view(ml_dtypes.float8_e4m3fn).astype(np.float64)
    else:
        nib = np.empty((g, p, n, 4), np.uint8)
        nib[..., 0::2] = words & 0xF
        nib[..., 1::2] = words >> 4
        vals = E2M1[nib]
    vals = vals * np.repeat(np.exp2(scales.astype(np.float64) - 127.0), 8, axis=1)[..., None]
    return vals.transpose(0, 1, 3, 2).reshape(g * 512, n)
def pack4(w):
    words, scales = pack_weight(w, "e2m1")
    return words.reshape(words.shape[0], 128, -1), scales


def unpack4(words, scales):
    return unpack_weight(words.reshape(words.shape[0], 128, -1, 2), scales, "e2m1")


M, KC, KE, F, B = 1024, 1024, 512, 1536, 512


def setup_inputs():
    s, u, t = mx_kscale(KC), mx_kscale(KE), mx_kscale(F)
    core = np.random.standard_normal((M, KC)) * s
    edge = np.random.standard_normal((M, KE)) * u
    core_taps = 0.8 * np.random.standard_normal((KC, F)) / np.sqrt(KC) / s[:, None]
    edge_taps = 0.6 * np.random.standard_normal((KE, F)) / np.sqrt(KE) / u[:, None]
    whiten = (1 + 0.1 * np.random.standard_normal(F)) * t
    combine = np.random.standard_normal((F, B)) / np.sqrt(F) / t[:, None]
    level = 0.5 * np.random.standard_normal(B)
    edge_taps_words, edge_taps_scales = pack4(edge_taps)
    combine_words, combine_scales = pack4(combine)
    return {"core": bf(core), "edge": bf(edge), "core_taps": bf(core_taps),
            "edge_taps_words": edge_taps_words, "edge_taps_scales": edge_taps_scales,
            "whiten": bf(whiten),
            "combine_words": combine_words, "combine_scales": combine_scales,
            "level": bf(level)}


def reference(core, edge, core_taps, edge_taps_words, edge_taps_scales, whiten, combine_words, combine_scales, level):
    y_core = mxq(f64(core), 1, "e4m3") @ mxq(f64(core_taps), 0, "e4m3")
    y_edge = mxq(f64(edge), 1, "e4m3") @ unpack4(edge_taps_words, edge_taps_scales)
    y = y_core + y_edge
    e = np.square(y) * f64(whiten)
    z = mxq(e, 1, "e4m3") @ unpack4(combine_words, combine_scales)
    return z - f64(level)

@@ -1,0 +1,545 @@
+from contextlib import ExitStack
+
+import concourse.mybir as mybir
+from concourse.masks import make_identity
+
+FRAMES, CORE, EDGE, FILTERS, BANDS = 1024, 1024, 512, 1536, 512
+FLOPS = 2 * FRAMES * (CORE + EDGE) * FILTERS + 2 * FRAMES * FILTERS * BANDS
+
+F32 = mybir.dt.float32
+BF16 = mybir.dt.bfloat16
+I32 = mybir.dt.int32
+U32 = mybir.dt.uint32
+U8 = mybir.dt.uint8
+FP8X4 = mybir.dt.float8_e4m3fn_x4
+FP4X4 = mybir.dt.float4_e2m1fn_x4
+ALU = mybir.AluOpType
+ACT = mybir.ActivationFunctionType
+
+P = 128
+PACK = 4
+W = 512
+GROUPS = FILTERS // W
+HALVES = FRAMES // W
+CHUNKS = (CORE + EDGE) // W
+
+
+def tile_multitaper_band_sensing_s3_kernel(
+    tc, core, edge, core_taps, edge_taps_words, edge_taps_scales, whiten, combine_words, combine_scales, level, out
+):
+    nc = tc.nc
+    with ExitStack() as ctx:
+        keep = ctx.enter_context(tc.tile_pool(name="keep", bufs=1))
+        stage = ctx.enter_context(tc.tile_pool(name="stage", bufs=3))
+        psum = ctx.enter_context(tc.psum_pool(name="psum", bufs=1))
+        ctx.enter_context(tc.manual_schedule())
+
+        def kept(name, shape, dtype):
+            return keep.tile(shape, dtype, name=name, align_bytes=64)
+
+        identity = kept("identity", [P, P], F32)
+        warm = kept("warm", [P, 16], F32)
+        x_raw = kept("x_raw", [P, HALVES, CHUNKS, PACK, W], BF16)
+        x_codes = kept("x_codes", [P, HALVES, CHUNKS, W], U32)
+        x_scales = kept("x_scales", [P, HALVES, CHUNKS, W], U8)
+        taps_raw = kept("taps_raw", [P, GROUPS, 2, PACK, W], BF16)
+        taps_codes = kept("taps_codes", [P, GROUPS, 2, W], U32)
+        taps_scales = kept("taps_scales", [P, GROUPS, 2, W], U8)
+        v_raw = kept("v_raw", [P, GROUPS, 2 * W], U8)
+        v_words = kept("v_words", [P, GROUPS, 2 * W], U8)
+        v_scales_raw = kept("v_scales_raw", [P, GROUPS, W], U8)
+        v_scales = kept("v_scales", [P, GROUPS, W], U8)
+        c_words = kept("c_words", [P, GROUPS, 2 * W], U8)
+        c_scales = kept("c_scales", [P, GROUPS, W], U8)
+        gain = kept("gain", [P, GROUPS, PACK], BF16)
+        gain_sign = kept("gain_sign", [P, GROUPS * PACK], F32)
+        gain_size = kept("gain_size", [P, GROUPS * PACK], F32)
+        gain_root = kept("gain_root", [P, GROUPS * PACK], F32)
+        half = kept("half", [P, GROUPS * PACK], F32)
+        ones = kept("ones", [P, P, PACK], BF16)
+        ones_codes = kept("ones_codes", [P, P], U32)
+        ones_scales = kept("ones_scales", [P, P], U8)
+        level_rows = kept("level_rows", [P, BANDS], BF16)
+        e_codes = kept("e_codes", [P, HALVES, GROUPS, W], U32)
+        e_scales = kept("e_scales", [P, HALVES, GROUPS, W], U8)
+        result = kept("result", [P, HALVES, PACK, BANDS], F32)
+        live = {}
+        free_banks = list(range(8))
+
+        def take_bank(key, shape):
+            number = free_banks[0]
+            free_banks.remove(number)
+            live[key] = psum.tile(shape, F32, name="bank", tag="bank%d" % number)
+            live["number", key] = number
+            return live[key]
+
+        def give_bank(key):
+            free_banks.append(live["number", key])
+            return live[key]
+
+        def copy_on(engine, out, in_):
+            if engine == "scalar":
+                nc.scalar.copy(out=out, in_=in_)
+            else:
+                nc.vector.tensor_copy(out=out, in_=in_)
+
+        def setup():
+            nc.scalar.dma_start(out=gain[:], in_=whiten.rearrange("(g p t) -> p g t", p=P, t=PACK))
+            nc.vector.memset(v_scales_raw[:].bitcast(I32), 0)
+            nc.vector.memset(ones[:], 1.0)
+            nc.vector.memset(warm[:, 0:8], 0.0)
+            quantize(ones_codes[:], ones_scales[:], ones[:])
+            nc.vector.memset(c_scales[:].bitcast(I32), 0)
+            make_identity(nc, identity[:])
+            nc.scalar.activation(out=warm[:, 8:16], in_=warm[:, 0:8], func=ACT.Square)
+            flat = gain[:].rearrange("p g t -> p (g t)")
+            nc.gpsimd.memset(half[:], 0.5)
+            nc.gpsimd.tensor_scalar(out=gain_size[:], in0=flat, scalar1=0.0, scalar2=-2.0, op0=ALU.is_lt, op1=ALU.mult)
+            nc.gpsimd.tensor_scalar(out=gain_sign[:], in0=gain_size[:], scalar1=1.0, scalar2=1.0, op0=ALU.mult, op1=ALU.add)
+            nc.gpsimd.tensor_tensor(out=gain_size[:], in0=flat, in1=gain_sign[:], op=ALU.mult)
+            nc.gpsimd.tensor_tensor(out=gain_root[:], in0=gain_size[:], in1=half[:], op=ALU.pow)
+
+        def warm_up(passes):
+            bank = take_bank("warm", [P, P])
+            for n in range(passes):
+                nc.tensor.matmul_mx(
+                    out=bank[:],
+                    lhsT=ones_codes[:].bitcast(FP8X4),
+                    lhsT_scale=ones_scales[:],
+                    rhs=ones_codes[:].bitcast(FP8X4),
+                    rhs_scale=ones_scales[:],
+                    start=True,
+                    stop=True,
+                )
+            give_bank("warm")
+
+        def load_samples(h, s):
+            columns = edge if s == 0 else core[:, (s - 1) * W : s * W]
+            rows = columns[h * W : (h + 1) * W, :].rearrange("(r i) k -> r i k", i=PACK)
+            nc.sync.dma_start(out=x_raw[:, h, s], in_=rows)
+
+        def load_taps(g, c):
+            rows = core_taps[c * W : (c + 1) * W, g * W : (g + 1) * W].rearrange("(p j) f -> p j f", j=PACK)
+            nc.sync.dma_start(out=taps_raw[:, g, c], in_=rows)
+
+        def load_v_words(g):
+            words = edge_taps_words[0][:, 2 * W * g : 2 * W * (g + 1)]
+            nc.sync.dma_start(out=v_raw[:, g].bitcast(I32), in_=words.bitcast(I32))
+
+        def load_v_scales():
+            plane = v_scales_raw[:].rearrange("p g n -> p (g n)").bitcast(I32)
+            for q in range(4):
+                nc.sync.dma_start(out=plane[32 * q : 32 * q + 4, :], in_=edge_taps_scales[0][4 * q : 4 * q + 4, :].bitcast(I32))
+
+        def load_combine_words():
+            nc.sync.dma_start(out=c_words[:].bitcast(I32), in_=combine_words.rearrange("g p n -> p g n").bitcast(I32))
+
+        def load_combine_scales():
+            for q in range(4):
+                rows = combine_scales[:, 4 * q : 4 * q + 4, :].rearrange("g r n -> r g n")
+                nc.sync.dma_start(out=c_scales[32 * q : 32 * q + 4].bitcast(I32), in_=rows.bitcast(I32))
+
+        def load_level():
+            nc.sync.dma_start(out=level_rows[:], in_=level.partition_broadcast(P))
+
+        def order_v_words(g):
+            nc.vector.tensor_copy(
+                out=v_words[:, g].rearrange("p (t m b) -> p t m b", t=PACK, b=2),
+                in_=v_raw[:, g].rearrange("p (m t b) -> p t m b", t=PACK, b=2),
+            )
+
+        def order_v_scales(g):
+            nc.vector.tensor_copy(
+                out=v_scales[:, g].rearrange("p (t m) -> p t m", t=PACK),
+                in_=v_scales_raw[:, g].rearrange("p (m t) -> p t m", t=PACK),
+            )
+
+        def transpose(h, s, pair):
+            turned = take_bank(("turned", h, s, pair), [P, 2, 2, P])
+            words = x_raw[:, h, s].bitcast(F32)
+            for i in range(2):
+                for u in range(2):
+                    nc.tensor.transpose(turned[:, i, u, :], words[:, 2 * pair + i, u : 2 * P : 2], identity[:])
+
+        def unload(h, s, pair, engine):
+            if ("x", h, s) not in live:
+                live["x", h, s] = stage.tile([P, W, PACK], BF16, name="x_grouped", bufs=4, align_bytes=64)
+            words = live["x", h, s][:].rearrange("p n t -> p (n t)").bitcast(F32)[:, pair * W : (pair + 1) * W]
+            copy_on(
+                engine,
+                words.rearrange("p (i r u) -> p i r u", i=2, u=2),
+                give_bank(("turned", h, s, pair))[:].rearrange("p i u r -> p i r u"),
+            )
+
+        def quantize(codes, scales, grouped):
+            nc.vector.quantize_mx(out=codes.bitcast(FP8X4), scales=scales, in_=grouped.rearrange("p n t -> p (n t)"))
+
+        def quantize_samples(h, s):
+            quantize(x_codes[:, h, s], x_scales[:, h, s], live["x", h, s][:])
+
+        def group_taps(g, c, t0, t1, engine):
+            if ("taps", g, c) not in live:
+                live["taps", g, c] = stage.tile([P, W, PACK], BF16, name="taps_grouped", bufs=4, align_bytes=64)
+            copy_on(
+                engine,
+                live["taps", g, c][:].rearrange("p (t a b) j -> p t a j b", t=PACK, b=2)[:, t0:t1],
+                taps_raw[:, g, c].rearrange("p j (a b t) -> p t a j b", t=PACK, b=2)[:, t0:t1],
+            )
+
+        def quantize_taps(g, c):
+            quantize(taps_codes[:, g, c], taps_scales[:, g, c], live["taps", g, c][:])
+
+        def filter_pass(h, g, t, s):
+            if s == 0:
+                take_bank(("y", h, g, t), [P, W])
+                codes = v_words[:, g, 2 * P * t : 2 * P * (t + 1)].bitcast(FP4X4)
+                scales = v_scales[:, g, P * t : P * (t + 1)]
+            else:
+                codes = taps_codes[:, g, s - 1, P * t : P * (t + 1)].bitcast(FP8X4)
+                scales = taps_scales[:, g, s - 1, P * t : P * (t + 1)]
+            nc.tensor.matmul_mx(
+                out=live["y", h, g, t][:],
+                lhsT=codes,
+                lhsT_scale=scales,
+                rhs=x_codes[:, h, s].bitcast(FP8X4),
+                rhs_scale=x_scales[:, h, s],
+                start=(s == 0),
+                stop=(s == CHUNKS - 1),
+            )
+
+        def filter_tile(h, g, t):
+            for s in range(CHUNKS):
+                filter_pass(h, g, t, s)
+
+        def square_scaled(h, g, t):
+            if ("squares", h, g) not in live:
+                live["squares", h, g] = stage.tile([P, PACK, W], BF16, name="squares", bufs=4)
+            column = PACK * g + t
+            nc.scalar.activation(
+                out=live["squares", h, g][:, t, :],
+                in_=give_bank(("y", h, g, t))[:],
+                func=ACT.Square,
+                scale=gain_root[:, column : column + 1],
+            )
+
+        def sign_energy(h, g, t):
+            column = PACK * g + t
+            rows = live["squares", h, g][:, t, :]
+            nc.vector.tensor_scalar(
+                out=rows, in0=rows, scalar1=gain_sign[:, column : column + 1], scalar2=None, op0=ALU.mult
+            )
+
+        def group_energy(h, g, n0, n1, engine):
+            if ("e", h, g) not in live:
+                live["e", h, g] = stage.tile([P, W, PACK], BF16, name="e_grouped", align_bytes=64)
+            copy_on(
+                engine,
+                live["e", h, g][:, n0:n1, :].rearrange("p (a b) t -> p a t b", b=4),
+                live["squares", h, g][:, :, n0:n1].rearrange("p t (a b) -> p a t b", b=4),
+            )
+
+        def square(h, g, t):
+            if ("squares", h, g) not in live:
+                live["squares", h, g] = stage.tile([P, PACK, W], F32, name="squares", bufs=4)
+            nc.scalar.activation(out=live["squares", h, g][:, t, :], in_=give_bank(("y", h, g, t))[:], func=ACT.Square)
+
+        def whiten_energy(h, g, n0, n1):
+            if ("e", h, g) not in live:
+                live["e", h, g] = stage.tile([P, W, PACK], BF16, name="e_grouped", align_bytes=64)
+            nc.vector.tensor_tensor(
+                out=live["e", h, g][:, n0:n1, :].rearrange("p (a b) t -> p a t b", b=2),
+                in0=live["squares", h, g][:, :, n0:n1].rearrange("p t (a b) -> p a t b", b=2),
+                in1=gain[:, g, :].unsqueeze(1).unsqueeze(3).to_broadcast([P, (n1 - n0) // 2, PACK, 2]),
+                op=ALU.mult,
+            )
+
+        def filter_narrow(h, g, i):
+            bank = take_bank(("y4", h, g, i), [P, PACK, P])
+            frames = slice(P * i, P * (i + 1))
+            for t in range(PACK):
+                for s in range(CHUNKS):
+                    if s == 0:
+                        codes = v_words[:, g, 2 * P * t : 2 * P * (t + 1)].bitcast(FP4X4)
+                        scales = v_scales[:, g, P * t : P * (t + 1)]
+                    else:
+                        codes = taps_codes[:, g, s - 1, P * t : P * (t + 1)].bitcast(FP8X4)
+                        scales = taps_scales[:, g, s - 1, P * t : P * (t + 1)]
+                    nc.tensor.matmul_mx(
+                        out=bank[:, t, :],
+                        lhsT=codes,
+                        lhsT_scale=scales,
+                        rhs=x_codes[:, h, s, frames].bitcast(FP8X4),
+                        rhs_scale=x_scales[:, h, s, frames],
+                        start=(s == 0),
+                        stop=(s == CHUNKS - 1),
+                    )
+
+        def square_narrow(h, g, i):
+            if ("squares", h, g) not in live:
+                live["squares", h, g] = stage.tile([P, W, PACK], F32, name="squares", bufs=4)
+            nc.scalar.activation(
+                out=live["squares", h, g][:, P * i : P * (i + 1), :],
+                in_=give_bank(("y4", h, g, i))[:].rearrange("p t n -> p n t"),
+                func=ACT.Square,
+            )
+
+        def whiten_narrow(h, g, i):
+            if ("e", h, g) not in live:
+                live["e", h, g] = stage.tile([P, W, PACK], BF16, name="e_grouped", align_bytes=64)
+            nc.vector.tensor_tensor(
+                out=live["e", h, g][:, P * i : P * (i + 1), :],
+                in0=live["squares", h, g][:, P * i : P * (i + 1), :],
+                in1=gain[:, g, :].unsqueeze(1).to_broadcast([P, P, PACK]),
+                op=ALU.mult,
+            )
+
+        def quantize_energy(h, g, n0, n1):
+            quantize(e_codes[:, h, g, n0:n1], e_scales[:, h, g, n0:n1], live["e", h, g][:, n0:n1, :])
+
+        def band_pass(h, i, g):
+            if g == 0:
+                take_bank(("z", h, i), [P, BANDS])
+            nc.tensor.matmul_mx(
+                out=live["z", h, i][:],
+                lhsT=e_codes[:, h, g, P * i : P * (i + 1)].bitcast(FP8X4),
+                lhsT_scale=e_scales[:, h, g, P * i : P * (i + 1)],
+                rhs=c_words[:, g].bitcast(FP4X4),
+                rhs_scale=c_scales[:, g],
+                start=(g == 0),
+                stop=(g == GROUPS - 1),
+            )
+
+        def subtract_level(h, i):
+            nc.vector.tensor_tensor(out=result[:, h, i], in0=give_bank(("z", h, i))[:], in1=level_rows[:], op=ALU.subtract)
+
+        def store(h, i):
+            rows = out[h * W : (h + 1) * W, :].rearrange("(r i) b -> r i b", i=PACK)
+            nc.sync.dma_start(out=rows[:, i, :], in_=result[:, h, i])
+
+        setup()
+        warm_up(14)
+        load_v_words(0)
+        order_v_words(0)
+        load_samples(0, 0)
+        load_v_scales()
+        order_v_scales(1)
+        order_v_scales(2)
+        order_v_scales(0)
+        transpose(0, 0, 0)
+        unload(0, 0, 0, "scalar")
+        transpose(0, 0, 1)
+        unload(0, 0, 1, "scalar")
+        quantize_samples(0, 0)
+        load_samples(0, 1)
+        transpose(0, 1, 0)
+        unload(0, 1, 0, "vector")
+        transpose(0, 1, 1)
+        filter_pass(0, 0, 0, 0)
+        filter_pass(0, 0, 1, 0)
+        load_taps(0, 0)
+        group_taps(0, 0, 0, 2, "scalar")
+        group_taps(0, 0, 2, 4, "vector")
+        filter_pass(0, 0, 2, 0)
+        quantize_taps(0, 0)
+        unload(0, 1, 1, "scalar")
+        load_samples(0, 2)
+        transpose(0, 2, 0)
+        transpose(0, 2, 1)
+        unload(0, 2, 1, "scalar")
+        quantize_samples(0, 1)
+        load_samples(1, 0)
+        transpose(1, 0, 0)
+        load_taps(0, 1)
+        group_taps(0, 1, 2, 4, "scalar")
+        load_samples(1, 1)
+        load_taps(1, 0)
+        filter_pass(0, 0, 0, 1)
+        filter_pass(0, 0, 1, 1)
+        filter_pass(0, 0, 3, 0)
+        filter_pass(0, 0, 3, 1)
+        unload(0, 2, 0, "vector")
+        unload(1, 0, 0, "scalar")
+        quantize_samples(0, 2)
+        transpose(1, 0, 1)
+        transpose(1, 1, 0)
+        group_taps(0, 1, 0, 2, "vector")
+        load_v_words(1)
+        quantize_taps(0, 1)
+        unload(1, 1, 0, "vector")
+        load_samples(1, 2)
+        unload(1, 0, 1, "scalar")
+        transpose(1, 1, 1)
+        load_taps(1, 1)
+        load_taps(2, 0)
+        load_v_words(2)
+        quantize_samples(1, 0)
+        unload(1, 1, 1, "vector")
+        filter_pass(0, 0, 0, 2)
+        filter_pass(0, 0, 3, 2)
+        group_taps(1, 0, 0, 2, "scalar")
+        filter_pass(0, 0, 2, 1)
+        filter_pass(0, 0, 1, 2)
+        square_scaled(0, 0, 0)
+        filter_pass(0, 0, 2, 2)
+        square_scaled(0, 0, 2)
+        transpose(1, 2, 0)
+        unload(1, 2, 0, "scalar")
+        group_taps(1, 0, 2, 4, "vector")
+        order_v_words(1)
+        transpose(1, 2, 1)
+        unload(1, 2, 1, "scalar")
+        filter_pass(1, 0, 1, 0)
+        filter_pass(1, 0, 0, 0)
+        quantize_samples(1, 1)
+        filter_pass(1, 0, 2, 0)
+        group_taps(1, 1, 0, 2, "vector")
+        group_taps(1, 1, 2, 4, "scalar")
+        filter_pass(1, 0, 1, 1)
+        square_scaled(0, 0, 3)
+        quantize_samples(1, 2)
+        filter_pass(1, 0, 3, 0)
+        square_scaled(0, 0, 1)
+        quantize_taps(1, 0)
+        quantize_taps(1, 1)
+        load_taps(2, 1)
+        filter_pass(1, 0, 2, 1)
+        filter_pass(1, 0, 3, 1)
+        filter_pass(1, 0, 0, 1)
+        sign_energy(0, 0, 3)
+        filter_pass(1, 0, 0, 2)
+        group_taps(2, 0, 2, 4, "vector")
+        sign_energy(0, 0, 2)
+        filter_pass(1, 0, 1, 2)
+        sign_energy(0, 0, 1)
+        order_v_words(2)
+        square_scaled(1, 0, 1)
+        sign_energy(0, 0, 0)
+        group_taps(2, 0, 0, 2, "vector")
+        sign_energy(1, 0, 1)
+        square_scaled(1, 0, 0)
+        sign_energy(1, 0, 0)
+        filter_pass(1, 0, 2, 2)
+        filter_pass(1, 0, 3, 2)
+        filter_tile(0, 1, 3)
+        square_scaled(1, 0, 2)
+        group_taps(2, 1, 2, 4, "scalar")
+        group_energy(0, 0, 256, 512, "vector")
+        filter_tile(0, 1, 2)
+        filter_tile(0, 1, 0)
+        sign_energy(1, 0, 2)
+        group_taps(2, 1, 0, 2, "scalar")
+        group_energy(0, 0, 0, 256, "vector")
+        square_scaled(1, 0, 3)
+        quantize_taps(2, 0)
+        square_scaled(0, 1, 2)
+        quantize_taps(2, 1)
+        filter_tile(0, 1, 1)
+        sign_energy(1, 0, 3)
+        quantize_energy(0, 0, 256, 512)
+        square_scaled(0, 1, 3)
+        square_scaled(0, 1, 0)
+        square_scaled(0, 1, 1)
+        filter_tile(1, 1, 3)
+        filter_tile(1, 1, 2)
+        filter_tile(1, 1, 1)
+        group_energy(1, 0, 256, 512, "vector")
+        sign_energy(0, 1, 2)
+        sign_energy(0, 1, 3)
+        load_combine_words()
+        filter_tile(0, 2, 2)
+        group_energy(1, 0, 0, 256, "vector")
+        filter_tile(0, 2, 3)
+        filter_tile(0, 2, 1)
+        filter_tile(0, 2, 0)
+        quantize_energy(0, 0, 0, 256)
+        square_scaled(1, 1, 1)
+        sign_energy(0, 1, 1)
+        sign_energy(1, 1, 1)
+        load_combine_scales()
+        sign_energy(0, 1, 0)
+        quantize_energy(1, 0, 0, 256)
+        quantize_energy(1, 0, 256, 512)
+        filter_tile(1, 2, 3)
+        square_scaled(0, 2, 2)
+        sign_energy(0, 2, 2)
+        filter_tile(1, 1, 0)
+        square_scaled(0, 2, 3)
+        square_scaled(1, 1, 2)
+        group_energy(0, 1, 0, 256, "vector")
+        sign_energy(0, 2, 3)
+        sign_energy(1, 1, 2)
+        group_energy(0, 1, 256, 512, "vector")
+        square_scaled(0, 2, 1)
+        sign_energy(0, 2, 1)
+        square_scaled(0, 2, 0)
+        square_scaled(1, 1, 3)
+        square_scaled(1, 1, 0)
+        sign_energy(0, 2, 0)
+        group_energy(0, 2, 0, 256, "scalar")
+        band_pass(0, 2, 0)
+        quantize_energy(0, 1, 0, 256)
+        quantize_energy(0, 1, 256, 512)
+        band_pass(0, 3, 0)
+        group_energy(0, 2, 256, 512, "vector")
+        sign_energy(1, 1, 3)
+        filter_tile(1, 2, 0)
+        square_scaled(1, 2, 0)
+        load_level()
+        sign_energy(1, 1, 0)
+        quantize_energy(0, 2, 256, 512)
+        square_scaled(1, 2, 3)
+        group_energy(1, 1, 256, 512, "vector")
+        band_pass(0, 2, 1)
+        filter_tile(1, 2, 2)
+        square_scaled(1, 2, 2)
+        band_pass(0, 3, 1)
+        band_pass(0, 3, 2)
+        quantize_energy(0, 2, 0, 256)
+        quantize_energy(1, 1, 256, 512)
+        subtract_level(0, 3)
+        filter_tile(1, 2, 1)
+        store(0, 3)
+        band_pass(0, 2, 2)
+        band_pass(0, 1, 0)
+        sign_energy(1, 2, 0)
+        band_pass(0, 1, 1)
+        band_pass(0, 1, 2)
+        sign_energy(1, 2, 3)
+        sign_energy(1, 2, 2)
+        square_scaled(1, 2, 1)
+        band_pass(1, 3, 0)
+        subtract_level(0, 2)
+        sign_energy(1, 2, 1)
+        group_energy(1, 1, 0, 256, "scalar")
+        group_energy(1, 2, 256, 512, "scalar")
+        subtract_level(0, 1)
+        band_pass(1, 2, 0)
+        store(0, 1)
+        band_pass(1, 0, 0)
+        group_energy(1, 2, 0, 256, "vector")
+        store(0, 2)
+        quantize_energy(1, 1, 0, 256)
+        band_pass(1, 2, 1)
+        quantize_energy(1, 2, 0, 256)
+        band_pass(0, 0, 0)
+        band_pass(0, 0, 1)
+        band_pass(0, 0, 2)
+        subtract_level(0, 0)
+        store(0, 0)
+        band_pass(1, 1, 0)
+        band_pass(1, 0, 1)
+        quantize_energy(1, 2, 256, 512)
+        band_pass(1, 0, 2)
+        subtract_level(1, 0)
+        band_pass(1, 1, 1)
+        band_pass(1, 1, 2)
+        subtract_level(1, 1)
+        band_pass(1, 3, 1)
+        store(1, 0)
+        store(1, 1)
+        band_pass(1, 2, 2)
+        subtract_level(1, 2)
+        store(1, 2)
+        band_pass(1, 3, 2)
+        subtract_level(1, 3)
+        store(1, 3)

@@ -39,10 +39,11 @@ def tile_multitaper_band_sensing_s3_kernel(
 
         identity = kept("identity", [P, P], F32)
         warm = kept("warm", [P, 16], F32)
-        x_raw = kept("x_raw", [P, HALVES, CHUNKS, PACK, W], BF16)
+        edge_raw = kept("edge_raw", [P, HALVES, PACK, EDGE], BF16)
+        core_raw = kept("core_raw", [P, HALVES, PACK, CORE], BF16)
         x_codes = kept("x_codes", [P, HALVES, CHUNKS, W], U32)
         x_scales = kept("x_scales", [P, HALVES, CHUNKS, W], U8)
-        taps_raw = kept("taps_raw", [P, GROUPS, 2, PACK, W], BF16)
+        taps_raw = kept("taps_raw", [P, 2, PACK, FILTERS], BF16)
         taps_codes = kept("taps_codes", [P, GROUPS, 2, W], U32)
         taps_scales = kept("taps_scales", [P, GROUPS, 2, W], U8)
         v_raw = kept("v_raw", [P, GROUPS, 2 * W], U8)
@@ -94,9 +95,8 @@ def tile_multitaper_band_sensing_s3_kernel(
             nc.scalar.activation(out=warm[:, 8:16], in_=warm[:, 0:8], func=ACT.Square)
             flat = gain[:].rearrange("p g t -> p (g t)")
             nc.gpsimd.memset(half[:], 0.5)
-            nc.gpsimd.tensor_scalar(out=gain_size[:], in0=flat, scalar1=0.0, scalar2=-2.0, op0=ALU.is_lt, op1=ALU.mult)
-            nc.gpsimd.tensor_scalar(out=gain_sign[:], in0=gain_size[:], scalar1=1.0, scalar2=1.0, op0=ALU.mult, op1=ALU.add)
-            nc.gpsimd.tensor_tensor(out=gain_size[:], in0=flat, in1=gain_sign[:], op=ALU.mult)
+            nc.scalar.activation(out=gain_size[:], in_=flat, func=ACT.Abs)
+            nc.scalar.activation(out=gain_sign[:], in_=flat, func=ACT.Sign)
             nc.gpsimd.tensor_tensor(out=gain_root[:], in0=gain_size[:], in1=half[:], op=ALU.pow)
 
         def warm_up(passes):
@@ -113,18 +113,22 @@ def tile_multitaper_band_sensing_s3_kernel(
                 )
             give_bank("warm")
 
-        def load_samples(h, s):
-            columns = edge if s == 0 else core[:, (s - 1) * W : s * W]
-            rows = columns[h * W : (h + 1) * W, :].rearrange("(r i) k -> r i k", i=PACK)
-            nc.sync.dma_start(out=x_raw[:, h, s], in_=rows)
+        def load_edge(h, i0, i1):
+            rows = edge[h * W : (h + 1) * W, :].rearrange("(r i) k -> r i k", i=PACK)
+            nc.sync.dma_start(out=edge_raw[:, h, i0:i1, :], in_=rows[:, i0:i1, :])
 
-        def load_taps(g, c):
-            rows = core_taps[c * W : (c + 1) * W, g * W : (g + 1) * W].rearrange("(p j) f -> p j f", j=PACK)
-            nc.sync.dma_start(out=taps_raw[:, g, c], in_=rows)
+        def load_core(h, i0, i1, c0, c1):
+            rows = core[h * W : (h + 1) * W, c0 * W : c1 * W].rearrange("(r i) k -> r i k", i=PACK)
+            nc.sync.dma_start(out=core_raw[:, h, i0:i1, c0 * W : c1 * W], in_=rows[:, i0:i1, :])
 
-        def load_v_words(g):
-            words = edge_taps_words[0][:, 2 * W * g : 2 * W * (g + 1)]
-            nc.sync.dma_start(out=v_raw[:, g].bitcast(I32), in_=words.bitcast(I32))
+        def load_taps(g0, g1, c):
+            rows = core_taps[c * W : (c + 1) * W, g0 * W : g1 * W].rearrange("(p j) f -> p j f", j=PACK)
+            nc.sync.dma_start(out=taps_raw[:, c, :, g0 * W : g1 * W], in_=rows)
+
+        def load_v_words(g0, g1):
+            words = edge_taps_words[0][:, 2 * W * g0 : 2 * W * g1]
+            target = v_raw[:, g0:g1].rearrange("p g n -> p (g n)")
+            nc.sync.dma_start(out=target.bitcast(I32), in_=words.bitcast(I32))
 
         def load_v_scales():
             plane = v_scales_raw[:].rearrange("p g n -> p (g n)").bitcast(I32)
@@ -142,21 +146,22 @@ def tile_multitaper_band_sensing_s3_kernel(
         def load_level():
             nc.sync.dma_start(out=level_rows[:], in_=level.partition_broadcast(P))
 
-        def order_v_words(g):
+        def order_v_words(g0, g1):
             nc.vector.tensor_copy(
-                out=v_words[:, g].rearrange("p (t m b) -> p t m b", t=PACK, b=2),
-                in_=v_raw[:, g].rearrange("p (m t b) -> p t m b", t=PACK, b=2),
+                out=v_words[:, g0:g1].rearrange("p g (t m b) -> p g t m b", t=PACK, b=2),
+                in_=v_raw[:, g0:g1].rearrange("p g (m t b) -> p g t m b", t=PACK, b=2),
             )
 
-        def order_v_scales(g):
+        def order_v_scales():
             nc.vector.tensor_copy(
-                out=v_scales[:, g].rearrange("p (t m) -> p t m", t=PACK),
-                in_=v_scales_raw[:, g].rearrange("p (m t) -> p t m", t=PACK),
+                out=v_scales[:].rearrange("p g (t m) -> p g t m", t=PACK),
+                in_=v_scales_raw[:].rearrange("p g (m t) -> p g t m", t=PACK),
             )
 
         def transpose(h, s, pair):
             turned = take_bank(("turned", h, s, pair), [P, 2, 2, P])
-            words = x_raw[:, h, s].bitcast(F32)
+            samples = edge_raw[:, h] if s == 0 else core_raw[:, h, :, (s - 1) * W : s * W]
+            words = samples.bitcast(F32)
             for i in range(2):
                 for u in range(2):
                     nc.tensor.transpose(turned[:, i, u, :], words[:, 2 * pair + i, u : 2 * P : 2], identity[:])
@@ -183,7 +188,7 @@ def tile_multitaper_band_sensing_s3_kernel(
             copy_on(
                 engine,
                 live["taps", g, c][:].rearrange("p (t a b) j -> p t a j b", t=PACK, b=2)[:, t0:t1],
-                taps_raw[:, g, c].rearrange("p j (a b t) -> p t a j b", t=PACK, b=2)[:, t0:t1],
+                taps_raw[:, c, :, g * W : (g + 1) * W].rearrange("p j (a b t) -> p t a j b", t=PACK, b=2)[:, t0:t1],
             )
 
         def quantize_taps(g, c):
@@ -229,13 +234,25 @@ def tile_multitaper_band_sensing_s3_kernel(
                 out=rows, in0=rows, scalar1=gain_sign[:, column : column + 1], scalar2=None, op0=ALU.mult
             )
 
+        def scale_energy(h, g, t):
+            if ("scaled", h, g) not in live:
+                live["scaled", h, g] = stage.tile([P, PACK, W], BF16, name="scaled", bufs=2)
+            column = PACK * g + t
+            nc.vector.tensor_scalar(
+                out=live["scaled", h, g][:, t, :],
+                in0=live["squares", h, g][:, t, :],
+                scalar1=gain[:].rearrange("p g t -> p (g t)")[:, column : column + 1],
+                scalar2=None,
+                op0=ALU.mult,
+            )
+
         def group_energy(h, g, n0, n1, engine):
             if ("e", h, g) not in live:
                 live["e", h, g] = stage.tile([P, W, PACK], BF16, name="e_grouped", align_bytes=64)
             copy_on(
                 engine,
                 live["e", h, g][:, n0:n1, :].rearrange("p (a b) t -> p a t b", b=4),
-                live["squares", h, g][:, :, n0:n1].rearrange("p t (a b) -> p a t b", b=4),
+                live.get(("scaled", h, g), live["squares", h, g])[:, :, n0:n1].rearrange("p t (a b) -> p a t b", b=4),
             )
 
         def square(h, g, t):
@@ -309,237 +326,233 @@ def tile_multitaper_band_sensing_s3_kernel(
                 stop=(g == GROUPS - 1),
             )
 
-        def subtract_level(h, i):
-            nc.vector.tensor_tensor(out=result[:, h, i], in0=give_bank(("z", h, i))[:], in1=level_rows[:], op=ALU.subtract)
+        def subtract_level(h, i, n0, n1):
+            bank = give_bank(("z", h, i)) if n1 == BANDS else live["z", h, i]
+            nc.vector.tensor_tensor(
+                out=result[:, h, i, n0:n1], in0=bank[:, n0:n1], in1=level_rows[:, n0:n1], op=ALU.subtract
+            )
 
-        def store(h, i):
+        def store(h, i, n0, n1):
             rows = out[h * W : (h + 1) * W, :].rearrange("(r i) b -> r i b", i=PACK)
-            nc.sync.dma_start(out=rows[:, i, :], in_=result[:, h, i])
+            nc.sync.dma_start(out=rows[:, i, n0:n1], in_=result[:, h, i, n0:n1])
 
         setup()
-        warm_up(14)
-        load_v_words(0)
-        order_v_words(0)
-        load_samples(0, 0)
-        load_v_scales()
-        order_v_scales(1)
-        order_v_scales(2)
-        order_v_scales(0)
+        load_edge(0, 0, 2)
+        load_v_words(0, 1)
         transpose(0, 0, 0)
-        unload(0, 0, 0, "scalar")
+        unload(0, 0, 0, "vector")
+        load_edge(0, 2, 4)
         transpose(0, 0, 1)
+        load_core(0, 0, 4, 0, 1)
+        load_v_scales()
+        transpose(0, 1, 0)
+        transpose(0, 1, 1)
+        order_v_words(0, 1)
         unload(0, 0, 1, "scalar")
         quantize_samples(0, 0)
-        load_samples(0, 1)
-        transpose(0, 1, 0)
-        unload(0, 1, 0, "vector")
-        transpose(0, 1, 1)
-        filter_pass(0, 0, 0, 0)
+        unload(0, 1, 0, "scalar")
+        warm_up(4)
+        order_v_scales()
         filter_pass(0, 0, 1, 0)
-        load_taps(0, 0)
-        group_taps(0, 0, 0, 2, "scalar")
+        load_taps(0, 1, 0)
         group_taps(0, 0, 2, 4, "vector")
-        filter_pass(0, 0, 2, 0)
+        unload(0, 1, 1, "vector")
+        load_taps(0, 1, 1)
+        group_taps(0, 1, 2, 4, "vector")
+        load_core(0, 0, 4, 1, 2)
+        group_taps(0, 0, 0, 2, "scalar")
         quantize_taps(0, 0)
-        unload(0, 1, 1, "scalar")
-        load_samples(0, 2)
-        transpose(0, 2, 0)
-        transpose(0, 2, 1)
-        unload(0, 2, 1, "scalar")
-        quantize_samples(0, 1)
-        load_samples(1, 0)
-        transpose(1, 0, 0)
-        load_taps(0, 1)
-        group_taps(0, 1, 2, 4, "scalar")
-        load_samples(1, 1)
-        load_taps(1, 0)
-        filter_pass(0, 0, 0, 1)
-        filter_pass(0, 0, 1, 1)
+        filter_pass(0, 0, 0, 0)
         filter_pass(0, 0, 3, 0)
-        filter_pass(0, 0, 3, 1)
-        unload(0, 2, 0, "vector")
-        unload(1, 0, 0, "scalar")
-        quantize_samples(0, 2)
-        transpose(1, 0, 1)
-        transpose(1, 1, 0)
-        group_taps(0, 1, 0, 2, "vector")
-        load_v_words(1)
+        filter_pass(0, 0, 2, 0)
+        transpose(0, 2, 1)
+        group_taps(0, 1, 0, 2, "scalar")
         quantize_taps(0, 1)
-        unload(1, 1, 0, "vector")
-        load_samples(1, 2)
-        unload(1, 0, 1, "scalar")
+        load_edge(1, 0, 4)
+        transpose(0, 2, 0)
+        transpose(1, 0, 0)
+        transpose(1, 0, 1)
+        quantize_samples(0, 1)
+        filter_pass(0, 0, 1, 1)
+        load_v_words(1, 3)
+        filter_pass(0, 0, 3, 1)
+        unload(0, 2, 1, "scalar")
+        load_core(1, 0, 4, 0, 1)
+        unload(0, 2, 0, "scalar")
+        order_v_words(1, 3)
         transpose(1, 1, 1)
-        load_taps(1, 1)
-        load_taps(2, 0)
-        load_v_words(2)
-        quantize_samples(1, 0)
-        unload(1, 1, 1, "vector")
-        filter_pass(0, 0, 0, 2)
+        unload(1, 0, 0, "scalar")
+        transpose(1, 1, 0)
+        quantize_samples(0, 2)
         filter_pass(0, 0, 3, 2)
-        group_taps(1, 0, 0, 2, "scalar")
-        filter_pass(0, 0, 2, 1)
         filter_pass(0, 0, 1, 2)
-        square_scaled(0, 0, 0)
-        filter_pass(0, 0, 2, 2)
-        square_scaled(0, 0, 2)
-        transpose(1, 2, 0)
-        unload(1, 2, 0, "scalar")
-        group_taps(1, 0, 2, 4, "vector")
-        order_v_words(1)
-        transpose(1, 2, 1)
-        unload(1, 2, 1, "scalar")
+        unload(1, 0, 1, "scalar")
+        quantize_samples(1, 0)
         filter_pass(1, 0, 1, 0)
-        filter_pass(1, 0, 0, 0)
-        quantize_samples(1, 1)
         filter_pass(1, 0, 2, 0)
+        load_taps(1, 2, 1)
+        group_taps(1, 1, 2, 4, "vector")
+        unload(1, 1, 1, "scalar")
+        load_taps(1, 2, 0)
         group_taps(1, 1, 0, 2, "vector")
-        group_taps(1, 1, 2, 4, "scalar")
-        filter_pass(1, 0, 1, 1)
-        square_scaled(0, 0, 3)
-        quantize_samples(1, 2)
+        unload(1, 1, 0, "scalar")
+        filter_pass(0, 0, 0, 1)
+        filter_pass(0, 0, 0, 2)
         filter_pass(1, 0, 3, 0)
-        square_scaled(0, 0, 1)
-        quantize_taps(1, 0)
-        quantize_taps(1, 1)
-        load_taps(2, 1)
-        filter_pass(1, 0, 2, 1)
-        filter_pass(1, 0, 3, 1)
-        filter_pass(1, 0, 0, 1)
+        square_scaled(0, 0, 3)
+        filter_pass(1, 0, 0, 0)
+        load_core(1, 0, 4, 1, 2)
+        quantize_samples(1, 1)
+        filter_pass(0, 0, 2, 1)
+        filter_pass(0, 0, 2, 2)
         sign_energy(0, 0, 3)
-        filter_pass(1, 0, 0, 2)
-        group_taps(2, 0, 2, 4, "vector")
-        sign_energy(0, 0, 2)
-        filter_pass(1, 0, 1, 2)
+        filter_pass(1, 0, 1, 1)
+        square_scaled(0, 0, 1)
         sign_energy(0, 0, 1)
-        order_v_words(2)
-        square_scaled(1, 0, 1)
+        load_taps(2, 3, 1)
+        filter_pass(1, 0, 2, 1)
+        group_taps(1, 0, 0, 2, "scalar")
+        square_scaled(0, 0, 2)
+        group_taps(1, 0, 2, 4, "vector")
+        quantize_taps(1, 1)
+        quantize_taps(1, 0)
+        transpose(1, 2, 1)
+        square_scaled(0, 0, 0)
+        group_taps(2, 1, 2, 4, "vector")
         sign_energy(0, 0, 0)
-        group_taps(2, 0, 0, 2, "vector")
-        sign_energy(1, 0, 1)
-        square_scaled(1, 0, 0)
-        sign_energy(1, 0, 0)
-        filter_pass(1, 0, 2, 2)
-        filter_pass(1, 0, 3, 2)
-        filter_tile(0, 1, 3)
-        square_scaled(1, 0, 2)
-        group_taps(2, 1, 2, 4, "scalar")
-        group_energy(0, 0, 256, 512, "vector")
+        transpose(1, 2, 0)
+        filter_pass(1, 0, 3, 1)
+        unload(1, 2, 1, "scalar")
+        load_taps(2, 3, 0)
+        sign_energy(0, 0, 2)
+        group_taps(2, 1, 0, 2, "vector")
+        unload(1, 2, 0, "scalar")
+        quantize_samples(1, 2)
+        filter_pass(1, 0, 0, 1)
+        group_taps(2, 0, 2, 4, "scalar")
         filter_tile(0, 1, 2)
         filter_tile(0, 1, 0)
-        sign_energy(1, 0, 2)
-        group_taps(2, 1, 0, 2, "scalar")
-        group_energy(0, 0, 0, 256, "vector")
-        square_scaled(1, 0, 3)
-        quantize_taps(2, 0)
+        group_taps(2, 0, 0, 2, "vector")
         square_scaled(0, 1, 2)
         quantize_taps(2, 1)
         filter_tile(0, 1, 1)
-        sign_energy(1, 0, 3)
-        quantize_energy(0, 0, 256, 512)
-        square_scaled(0, 1, 3)
         square_scaled(0, 1, 0)
         square_scaled(0, 1, 1)
-        filter_tile(1, 1, 3)
-        filter_tile(1, 1, 2)
-        filter_tile(1, 1, 1)
-        group_energy(1, 0, 256, 512, "vector")
-        sign_energy(0, 1, 2)
-        sign_energy(0, 1, 3)
-        load_combine_words()
-        filter_tile(0, 2, 2)
-        group_energy(1, 0, 0, 256, "vector")
-        filter_tile(0, 2, 3)
-        filter_tile(0, 2, 1)
-        filter_tile(0, 2, 0)
-        quantize_energy(0, 0, 0, 256)
-        square_scaled(1, 1, 1)
-        sign_energy(0, 1, 1)
-        sign_energy(1, 1, 1)
         load_combine_scales()
-        sign_energy(0, 1, 0)
-        quantize_energy(1, 0, 0, 256)
-        quantize_energy(1, 0, 256, 512)
-        filter_tile(1, 2, 3)
-        square_scaled(0, 2, 2)
-        sign_energy(0, 2, 2)
-        filter_tile(1, 1, 0)
-        square_scaled(0, 2, 3)
-        square_scaled(1, 1, 2)
-        group_energy(0, 1, 0, 256, "vector")
-        sign_energy(0, 2, 3)
-        sign_energy(1, 1, 2)
-        group_energy(0, 1, 256, 512, "vector")
-        square_scaled(0, 2, 1)
-        sign_energy(0, 2, 1)
+        filter_pass(1, 0, 0, 2)
+        square_scaled(1, 0, 0)
+        filter_pass(1, 0, 2, 2)
+        square_scaled(1, 0, 2)
+        filter_tile(0, 1, 3)
+        filter_pass(1, 0, 3, 2)
+        sign_energy(0, 1, 2)
+        filter_pass(1, 0, 1, 2)
+        square_scaled(0, 1, 3)
+        quantize_taps(2, 0)
+        filter_tile(0, 2, 2)
+        group_energy(0, 0, 0, 512, "vector")
+        filter_tile(0, 2, 0)
+        square_scaled(1, 0, 3)
+        square_scaled(1, 0, 1)
         square_scaled(0, 2, 0)
-        square_scaled(1, 1, 3)
+        sign_energy(0, 1, 1)
+        filter_tile(0, 2, 3)
+        square_scaled(0, 2, 3)
+        sign_energy(1, 0, 2)
+        filter_tile(0, 2, 1)
+        sign_energy(1, 0, 0)
+        quantize_energy(0, 0, 0, 512)
+        filter_tile(1, 1, 0)
+        square_scaled(0, 2, 2)
+        square_scaled(0, 2, 1)
+        sign_energy(0, 1, 0)
+        sign_energy(0, 1, 3)
         square_scaled(1, 1, 0)
+        sign_energy(1, 0, 3)
+        sign_energy(1, 0, 1)
+        group_energy(0, 1, 0, 512, "vector")
         sign_energy(0, 2, 0)
-        group_energy(0, 2, 0, 256, "scalar")
-        band_pass(0, 2, 0)
-        quantize_energy(0, 1, 0, 256)
-        quantize_energy(0, 1, 256, 512)
-        band_pass(0, 3, 0)
-        group_energy(0, 2, 256, 512, "vector")
-        sign_energy(1, 1, 3)
-        filter_tile(1, 2, 0)
-        square_scaled(1, 2, 0)
-        load_level()
-        sign_energy(1, 1, 0)
-        quantize_energy(0, 2, 256, 512)
-        square_scaled(1, 2, 3)
-        group_energy(1, 1, 256, 512, "vector")
-        band_pass(0, 2, 1)
+        quantize_energy(0, 1, 0, 512)
+        sign_energy(0, 2, 3)
+        filter_tile(1, 1, 2)
+        square_scaled(1, 1, 2)
+        sign_energy(0, 2, 1)
+        filter_tile(1, 1, 1)
+        sign_energy(0, 2, 2)
         filter_tile(1, 2, 2)
-        square_scaled(1, 2, 2)
-        band_pass(0, 3, 1)
-        band_pass(0, 3, 2)
+        sign_energy(1, 1, 0)
+        group_energy(0, 2, 0, 256, "vector")
+        sign_energy(1, 1, 2)
+        filter_tile(1, 1, 3)
+        group_energy(0, 2, 256, 512, "scalar")
+        group_energy(1, 0, 0, 512, "vector")
+        square_scaled(1, 1, 1)
         quantize_energy(0, 2, 0, 256)
-        quantize_energy(1, 1, 256, 512)
-        subtract_level(0, 3)
+        square_scaled(1, 1, 3)
+        sign_energy(1, 1, 1)
+        quantize_energy(0, 2, 256, 512)
+        square_scaled(1, 2, 2)
         filter_tile(1, 2, 1)
-        store(0, 3)
-        band_pass(0, 2, 2)
-        band_pass(0, 1, 0)
-        sign_energy(1, 2, 0)
-        band_pass(0, 1, 1)
-        band_pass(0, 1, 2)
-        sign_energy(1, 2, 3)
-        sign_energy(1, 2, 2)
+        filter_tile(1, 2, 3)
         square_scaled(1, 2, 1)
-        band_pass(1, 3, 0)
-        subtract_level(0, 2)
+        sign_energy(1, 1, 3)
+        quantize_energy(1, 0, 0, 512)
+        sign_energy(1, 2, 2)
+        group_energy(1, 1, 256, 512, "vector")
+        square_scaled(1, 2, 3)
+        filter_tile(1, 2, 0)
         sign_energy(1, 2, 1)
+        square_scaled(1, 2, 0)
+        sign_energy(1, 2, 3)
+        load_level()
+        quantize_energy(1, 1, 256, 512)
+        sign_energy(1, 2, 0)
         group_energy(1, 1, 0, 256, "scalar")
-        group_energy(1, 2, 256, 512, "scalar")
-        subtract_level(0, 1)
-        band_pass(1, 2, 0)
-        store(0, 1)
-        band_pass(1, 0, 0)
-        group_energy(1, 2, 0, 256, "vector")
-        store(0, 2)
-        quantize_energy(1, 1, 0, 256)
-        band_pass(1, 2, 1)
-        quantize_energy(1, 2, 0, 256)
+        load_combine_words()
+        band_pass(0, 1, 0)
+        band_pass(0, 3, 0)
+        band_pass(0, 1, 1)
+        band_pass(0, 2, 0)
+        band_pass(0, 1, 2)
+        band_pass(0, 2, 1)
+        band_pass(0, 2, 2)
+        group_energy(1, 2, 0, 256, "scalar")
+        subtract_level(0, 1, 0, 512)
+        store(0, 1, 0, 512)
+        subtract_level(0, 2, 0, 512)
+        store(0, 2, 0, 512)
         band_pass(0, 0, 0)
         band_pass(0, 0, 1)
+        group_energy(1, 2, 256, 512, "scalar")
+        quantize_energy(1, 1, 0, 256)
+        band_pass(0, 3, 1)
         band_pass(0, 0, 2)
-        subtract_level(0, 0)
-        store(0, 0)
+        band_pass(0, 3, 2)
+        band_pass(1, 2, 0)
+        band_pass(1, 0, 0)
         band_pass(1, 1, 0)
-        band_pass(1, 0, 1)
-        quantize_energy(1, 2, 256, 512)
-        band_pass(1, 0, 2)
-        subtract_level(1, 0)
+        subtract_level(0, 0, 0, 512)
         band_pass(1, 1, 1)
+        store(0, 0, 0, 512)
+        quantize_energy(1, 2, 0, 256)
+        band_pass(1, 0, 1)
+        band_pass(1, 0, 2)
+        subtract_level(0, 3, 0, 512)
+        store(0, 3, 0, 512)
+        quantize_energy(1, 2, 256, 512)
+        subtract_level(1, 0, 0, 512)
+        band_pass(1, 3, 0)
+        store(1, 0, 0, 512)
         band_pass(1, 1, 2)
-        subtract_level(1, 1)
+        subtract_level(1, 1, 0, 512)
         band_pass(1, 3, 1)
-        store(1, 0)
-        store(1, 1)
-        band_pass(1, 2, 2)
-        subtract_level(1, 2)
-        store(1, 2)
+        store(1, 1, 0, 512)
         band_pass(1, 3, 2)
-        subtract_level(1, 3)
-        store(1, 3)
+        subtract_level(1, 3, 0, 256)
+        subtract_level(1, 3, 256, 512)
+        store(1, 3, 0, 256)
+        store(1, 3, 256, 512)
+        band_pass(1, 2, 1)
+        band_pass(1, 2, 2)
+        subtract_level(1, 2, 0, 512)
+        store(1, 2, 0, 512)

@@ -337,221 +337,227 @@ def tile_multitaper_band_sensing_s3_kernel(
             nc.sync.dma_start(out=rows[:, i, n0:n1], in_=result[:, h, i, n0:n1])
 
         setup()
-        load_edge(0, 0, 2)
         load_v_words(0, 1)
-        transpose(0, 0, 0)
-        unload(0, 0, 0, "vector")
-        load_edge(0, 2, 4)
-        transpose(0, 0, 1)
-        load_core(0, 0, 4, 0, 1)
-        load_v_scales()
-        transpose(0, 1, 0)
-        transpose(0, 1, 1)
-        order_v_words(0, 1)
-        unload(0, 0, 1, "scalar")
-        quantize_samples(0, 0)
-        unload(0, 1, 0, "scalar")
         warm_up(4)
-        order_v_scales()
-        filter_pass(0, 0, 1, 0)
+        warm_up(4)
+        warm_up(4)
+        load_edge(1, 0, 4)
+        warm_up(4)
+        load_edge(0, 0, 2)
+        transpose(1, 0, 1)
+        unload(1, 0, 1, "vector")
+        load_edge(0, 2, 4)
+        transpose(1, 0, 0)
+        unload(1, 0, 0, "scalar")
+        warm_up(4)
+        load_v_scales()
+        warm_up(4)
+        transpose(0, 0, 0)
+        unload(0, 0, 0, "scalar")
+        order_v_words(0, 1)
+        load_core(0, 0, 2, 0, 2)
+        warm_up(4)
+        transpose(0, 0, 1)
+        load_core(0, 2, 4, 0, 2)
+        unload(0, 0, 1, "scalar")
         load_taps(0, 1, 0)
-        group_taps(0, 0, 2, 4, "vector")
-        unload(0, 1, 1, "vector")
-        load_taps(0, 1, 1)
-        group_taps(0, 1, 2, 4, "vector")
-        load_core(0, 0, 4, 1, 2)
-        group_taps(0, 0, 0, 2, "scalar")
-        quantize_taps(0, 0)
-        filter_pass(0, 0, 0, 0)
-        filter_pass(0, 0, 3, 0)
-        filter_pass(0, 0, 2, 0)
+        transpose(0, 1, 0)
+        quantize_samples(1, 0)
+        unload(0, 1, 0, "scalar")
+        load_core(1, 2, 4, 0, 2)
+        order_v_scales()
+        transpose(0, 1, 1)
+        quantize_samples(0, 0)
+        group_taps(0, 0, 0, 2, "vector")
+        unload(0, 1, 1, "scalar")
+        quantize_samples(0, 1)
         transpose(0, 2, 1)
+        filter_pass(1, 0, 1, 0)
+        filter_pass(1, 0, 3, 0)
+        transpose(0, 2, 0)
+        unload(0, 2, 1, "vector")
+        group_taps(0, 0, 2, 4, "scalar")
+        load_taps(0, 1, 1)
+        filter_pass(1, 0, 0, 0)
+        unload(0, 2, 0, "scalar")
+        filter_pass(0, 0, 3, 0)
+        load_core(1, 0, 2, 0, 2)
+        quantize_taps(0, 0)
+        group_taps(0, 1, 2, 4, "vector")
+        load_v_words(1, 3)
+        quantize_samples(0, 2)
+        transpose(1, 2, 1)
         group_taps(0, 1, 0, 2, "scalar")
         quantize_taps(0, 1)
-        load_edge(1, 0, 4)
-        transpose(0, 2, 0)
-        transpose(1, 0, 0)
-        transpose(1, 0, 1)
-        quantize_samples(0, 1)
-        filter_pass(0, 0, 1, 1)
-        load_v_words(1, 3)
-        filter_pass(0, 0, 3, 1)
-        unload(0, 2, 1, "scalar")
-        load_core(1, 0, 4, 0, 1)
-        unload(0, 2, 0, "scalar")
+        unload(1, 2, 1, "scalar")
         order_v_words(1, 3)
         transpose(1, 1, 1)
-        unload(1, 0, 0, "scalar")
-        transpose(1, 1, 0)
-        quantize_samples(0, 2)
-        filter_pass(0, 0, 3, 2)
-        filter_pass(0, 0, 1, 2)
-        unload(1, 0, 1, "scalar")
-        quantize_samples(1, 0)
-        filter_pass(1, 0, 1, 0)
-        filter_pass(1, 0, 2, 0)
-        load_taps(1, 2, 1)
-        group_taps(1, 1, 2, 4, "vector")
-        unload(1, 1, 1, "scalar")
         load_taps(1, 2, 0)
-        group_taps(1, 1, 0, 2, "vector")
-        unload(1, 1, 0, "scalar")
-        filter_pass(0, 0, 0, 1)
-        filter_pass(0, 0, 0, 2)
-        filter_pass(1, 0, 3, 0)
-        square_scaled(0, 0, 3)
-        filter_pass(1, 0, 0, 0)
-        load_core(1, 0, 4, 1, 2)
-        quantize_samples(1, 1)
+        unload(1, 1, 1, "scalar")
+        filter_pass(0, 0, 2, 0)
         filter_pass(0, 0, 2, 1)
-        filter_pass(0, 0, 2, 2)
-        sign_energy(0, 0, 3)
-        filter_pass(1, 0, 1, 1)
-        square_scaled(0, 0, 1)
-        sign_energy(0, 0, 1)
-        load_taps(2, 3, 1)
-        filter_pass(1, 0, 2, 1)
-        group_taps(1, 0, 0, 2, "scalar")
-        square_scaled(0, 0, 2)
-        group_taps(1, 0, 2, 4, "vector")
-        quantize_taps(1, 1)
-        quantize_taps(1, 0)
-        transpose(1, 2, 1)
-        square_scaled(0, 0, 0)
-        group_taps(2, 1, 2, 4, "vector")
-        sign_energy(0, 0, 0)
         transpose(1, 2, 0)
-        filter_pass(1, 0, 3, 1)
-        unload(1, 2, 1, "scalar")
-        load_taps(2, 3, 0)
-        sign_energy(0, 0, 2)
-        group_taps(2, 1, 0, 2, "vector")
+        transpose(1, 1, 0)
         unload(1, 2, 0, "scalar")
         quantize_samples(1, 2)
-        filter_pass(1, 0, 0, 1)
-        group_taps(2, 0, 2, 4, "scalar")
-        filter_tile(0, 1, 2)
-        filter_tile(0, 1, 0)
-        group_taps(2, 0, 0, 2, "vector")
-        square_scaled(0, 1, 2)
-        quantize_taps(2, 1)
-        filter_tile(0, 1, 1)
-        square_scaled(0, 1, 0)
-        square_scaled(0, 1, 1)
-        load_combine_scales()
-        filter_pass(1, 0, 0, 2)
-        square_scaled(1, 0, 0)
-        filter_pass(1, 0, 2, 2)
-        square_scaled(1, 0, 2)
-        filter_tile(0, 1, 3)
+        filter_pass(0, 0, 1, 0)
+        unload(1, 1, 0, "scalar")
+        group_taps(1, 0, 2, 4, "scalar")
+        filter_pass(0, 0, 3, 1)
+        filter_pass(0, 0, 3, 2)
+        load_taps(1, 2, 1)
+        group_taps(1, 1, 2, 4, "scalar")
+        quantize_samples(1, 1)
+        load_taps(2, 3, 0)
+        filter_pass(0, 0, 1, 1)
+        filter_pass(1, 0, 2, 0)
+        filter_pass(0, 0, 0, 0)
+        filter_pass(0, 0, 0, 1)
+        filter_pass(0, 0, 0, 2)
+        filter_pass(1, 0, 3, 1)
+        group_taps(1, 0, 0, 2, "vector")
         filter_pass(1, 0, 3, 2)
-        sign_energy(0, 1, 2)
-        filter_pass(1, 0, 1, 2)
-        square_scaled(0, 1, 3)
-        quantize_taps(2, 0)
-        filter_tile(0, 2, 2)
-        group_energy(0, 0, 0, 512, "vector")
-        filter_tile(0, 2, 0)
+        filter_pass(0, 0, 1, 2)
         square_scaled(1, 0, 3)
-        square_scaled(1, 0, 1)
-        square_scaled(0, 2, 0)
-        sign_energy(0, 1, 1)
-        filter_tile(0, 2, 3)
-        square_scaled(0, 2, 3)
-        sign_energy(1, 0, 2)
-        filter_tile(0, 2, 1)
-        sign_energy(1, 0, 0)
-        quantize_energy(0, 0, 0, 512)
-        filter_tile(1, 1, 0)
-        square_scaled(0, 2, 2)
-        square_scaled(0, 2, 1)
-        sign_energy(0, 1, 0)
-        sign_energy(0, 1, 3)
-        square_scaled(1, 1, 0)
+        group_taps(1, 1, 0, 2, "vector")
+        load_taps(2, 3, 1)
+        quantize_taps(1, 0)
+        quantize_taps(1, 1)
         sign_energy(1, 0, 3)
-        sign_energy(1, 0, 1)
-        group_energy(0, 1, 0, 512, "vector")
-        sign_energy(0, 2, 0)
-        quantize_energy(0, 1, 0, 512)
-        sign_energy(0, 2, 3)
-        filter_tile(1, 1, 2)
-        square_scaled(1, 1, 2)
-        sign_energy(0, 2, 1)
-        filter_tile(1, 1, 1)
-        sign_energy(0, 2, 2)
-        filter_tile(1, 2, 2)
-        sign_energy(1, 1, 0)
-        group_energy(0, 2, 0, 256, "vector")
-        sign_energy(1, 1, 2)
-        filter_tile(1, 1, 3)
-        group_energy(0, 2, 256, 512, "scalar")
-        group_energy(1, 0, 0, 512, "vector")
-        square_scaled(1, 1, 1)
-        quantize_energy(0, 2, 0, 256)
-        square_scaled(1, 1, 3)
-        sign_energy(1, 1, 1)
-        quantize_energy(0, 2, 256, 512)
-        square_scaled(1, 2, 2)
-        filter_tile(1, 2, 1)
-        filter_tile(1, 2, 3)
-        square_scaled(1, 2, 1)
-        sign_energy(1, 1, 3)
-        quantize_energy(1, 0, 0, 512)
-        sign_energy(1, 2, 2)
-        group_energy(1, 1, 256, 512, "vector")
-        square_scaled(1, 2, 3)
-        filter_tile(1, 2, 0)
-        sign_energy(1, 2, 1)
-        square_scaled(1, 2, 0)
-        sign_energy(1, 2, 3)
+        filter_pass(1, 0, 1, 1)
+        group_taps(2, 0, 2, 4, "vector")
+        load_combine_scales()
+        group_taps(2, 0, 0, 2, "vector")
+        filter_pass(0, 0, 2, 2)
+        square_scaled(0, 0, 2)
+        sign_energy(0, 0, 2)
+        filter_pass(1, 0, 1, 2)
+        filter_pass(1, 0, 2, 1)
+        filter_pass(1, 0, 0, 1)
+        filter_pass(1, 0, 2, 2)
+        group_taps(2, 1, 2, 4, "vector")
+        group_taps(2, 1, 0, 2, "vector")
+        filter_pass(1, 0, 0, 2)
+        filter_tile(0, 1, 3)
+        filter_tile(0, 1, 1)
+        quantize_taps(2, 0)
+        square_scaled(1, 0, 1)
+        square_scaled(0, 0, 1)
+        quantize_taps(2, 1)
+        sign_energy(0, 0, 1)
         load_level()
-        quantize_energy(1, 1, 256, 512)
-        sign_energy(1, 2, 0)
-        group_energy(1, 1, 0, 256, "scalar")
+        square_scaled(1, 0, 2)
+        square_scaled(1, 0, 0)
+        filter_tile(0, 1, 2)
         load_combine_words()
-        band_pass(0, 1, 0)
-        band_pass(0, 3, 0)
-        band_pass(0, 1, 1)
+        filter_tile(0, 1, 0)
+        square_scaled(0, 0, 3)
+        sign_energy(1, 0, 2)
+        filter_tile(1, 1, 0)
+        filter_tile(0, 2, 3)
+        square_scaled(0, 1, 1)
+        sign_energy(1, 0, 0)
+        sign_energy(0, 0, 3)
+        square_scaled(0, 0, 0)
+        filter_tile(0, 2, 0)
+        square_scaled(0, 1, 2)
+        sign_energy(1, 0, 1)
+        filter_tile(0, 2, 1)
+        square_scaled(0, 1, 3)
+        square_scaled(0, 1, 0)
+        filter_tile(0, 2, 2)
+        sign_energy(0, 0, 0)
+        sign_energy(0, 1, 1)
+        sign_energy(0, 1, 2)
+        square_scaled(0, 2, 3)
+        group_energy(1, 0, 0, 512, "vector")
+        sign_energy(0, 1, 3)
+        sign_energy(0, 1, 0)
+        quantize_energy(1, 0, 0, 512)
+        group_energy(0, 0, 0, 512, "vector")
+        filter_tile(1, 1, 3)
+        filter_tile(1, 2, 2)
+        sign_energy(0, 2, 3)
+        square_scaled(0, 2, 0)
+        sign_energy(0, 2, 0)
+        square_scaled(0, 2, 1)
+        sign_energy(0, 2, 1)
+        square_scaled(1, 1, 0)
+        sign_energy(1, 1, 0)
+        square_scaled(0, 2, 2)
+        sign_energy(0, 2, 2)
+        filter_tile(1, 1, 1)
+        square_scaled(1, 1, 3)
+        group_energy(0, 1, 0, 512, "vector")
+        sign_energy(1, 1, 3)
+        group_energy(0, 2, 0, 256, "vector")
+        square_scaled(1, 2, 2)
+        sign_energy(1, 2, 2)
+        group_energy(0, 2, 256, 512, "scalar")
+        filter_tile(1, 1, 2)
+        filter_tile(1, 2, 0)
+        square_scaled(1, 1, 1)
+        quantize_energy(0, 0, 0, 512)
+        square_scaled(1, 1, 2)
+        filter_tile(1, 2, 3)
+        square_scaled(1, 2, 0)
+        filter_tile(1, 2, 1)
+        band_pass(0, 0, 0)
+        sign_energy(1, 1, 1)
+        band_pass(1, 0, 0)
+        quantize_energy(0, 1, 0, 512)
+        quantize_energy(0, 2, 0, 256)
+        sign_energy(1, 1, 2)
+        quantize_energy(0, 2, 256, 512)
+        sign_energy(1, 2, 0)
+        square_scaled(1, 2, 3)
         band_pass(0, 2, 0)
-        band_pass(0, 1, 2)
         band_pass(0, 2, 1)
+        square_scaled(1, 2, 1)
         band_pass(0, 2, 2)
-        group_energy(1, 2, 0, 256, "scalar")
-        subtract_level(0, 1, 0, 512)
-        store(0, 1, 0, 512)
+        group_energy(1, 1, 0, 256, "vector")
+        sign_energy(1, 2, 3)
+        sign_energy(1, 2, 1)
+        group_energy(1, 1, 256, 512, "scalar")
+        quantize_energy(1, 1, 0, 256)
         subtract_level(0, 2, 0, 512)
         store(0, 2, 0, 512)
-        band_pass(0, 0, 0)
-        band_pass(0, 0, 1)
-        group_energy(1, 2, 256, 512, "scalar")
-        quantize_energy(1, 1, 0, 256)
+        band_pass(0, 3, 0)
         band_pass(0, 3, 1)
-        band_pass(0, 0, 2)
         band_pass(0, 3, 2)
-        band_pass(1, 2, 0)
-        band_pass(1, 0, 0)
-        band_pass(1, 1, 0)
+        group_energy(1, 2, 0, 256, "scalar")
+        group_energy(1, 2, 256, 512, "scalar")
+        subtract_level(0, 3, 0, 512)
+        band_pass(0, 0, 1)
+        band_pass(0, 0, 2)
         subtract_level(0, 0, 0, 512)
-        band_pass(1, 1, 1)
+        band_pass(0, 1, 0)
+        band_pass(0, 1, 1)
+        band_pass(0, 1, 2)
+        band_pass(1, 3, 0)
+        store(0, 3, 0, 512)
         store(0, 0, 0, 512)
         quantize_energy(1, 2, 0, 256)
+        subtract_level(0, 1, 0, 512)
+        quantize_energy(1, 1, 256, 512)
         band_pass(1, 0, 1)
         band_pass(1, 0, 2)
-        subtract_level(0, 3, 0, 512)
-        store(0, 3, 0, 512)
-        quantize_energy(1, 2, 256, 512)
         subtract_level(1, 0, 0, 512)
-        band_pass(1, 3, 0)
+        store(0, 1, 0, 512)
+        quantize_energy(1, 2, 256, 512)
+        band_pass(1, 1, 0)
         store(1, 0, 0, 512)
+        band_pass(1, 1, 1)
         band_pass(1, 1, 2)
         subtract_level(1, 1, 0, 512)
         band_pass(1, 3, 1)
+        band_pass(1, 2, 0)
         store(1, 1, 0, 512)
         band_pass(1, 3, 2)
-        subtract_level(1, 3, 0, 256)
         subtract_level(1, 3, 256, 512)
-        store(1, 3, 0, 256)
         store(1, 3, 256, 512)
+        subtract_level(1, 3, 0, 256)
+        store(1, 3, 0, 256)
         band_pass(1, 2, 1)
         band_pass(1, 2, 2)
         subtract_level(1, 2, 0, 512)

@@ -18,10 +18,26 @@ ACT = mybir.ActivationFunctionType
 
 P = 128
 PACK = 4
-W = 512
-GROUPS = FILTERS // W
+W = P * PACK
 HALVES = FRAMES // W
-CHUNKS = (CORE + EDGE) // W
+GROUPS = FILTERS // W
+CORE_CHUNKS = CORE // W
+CHUNKS = 1 + CORE_CHUNKS
+PSUM_BANKS = 8
+QUADRANT = 32
+SCALE_ROWS = 4
+
+ALL = slice(0, W)
+FIRST = slice(0, W // 2)
+SECOND = slice(W // 2, W)
+
+SAMPLE_BUFS = 4
+TAPS_BUFS = 4
+SQUARE_BUFS = 4
+ENERGY_BUFS = 3
+
+WARM_PASSES_AT_START = 16
+WARM_PASSES_BETWEEN_LOADS = 8
 
 
 def tile_multitaper_band_sensing_s3_kernel(
@@ -30,7 +46,7 @@ def tile_multitaper_band_sensing_s3_kernel(
     nc = tc.nc
     with ExitStack() as ctx:
         keep = ctx.enter_context(tc.tile_pool(name="keep", bufs=1))
-        stage = ctx.enter_context(tc.tile_pool(name="stage", bufs=3))
+        stage = ctx.enter_context(tc.tile_pool(name="stage", bufs=1))
         psum = ctx.enter_context(tc.psum_pool(name="psum", bufs=1))
         ctx.enter_context(tc.manual_schedule())
 
@@ -38,66 +54,77 @@ def tile_multitaper_band_sensing_s3_kernel(
             return keep.tile(shape, dtype, name=name, align_bytes=64)
 
         identity = kept("identity", [P, P], F32)
-        warm = kept("warm", [P, 16], F32)
+        table_probe = kept("table_probe", [P, 2, 8], F32)
         edge_raw = kept("edge_raw", [P, HALVES, PACK, EDGE], BF16)
         core_raw = kept("core_raw", [P, HALVES, PACK, CORE], BF16)
-        x_codes = kept("x_codes", [P, HALVES, CHUNKS, W], U32)
-        x_scales = kept("x_scales", [P, HALVES, CHUNKS, W], U8)
-        taps_raw = kept("taps_raw", [P, 2, PACK, FILTERS], BF16)
-        taps_codes = kept("taps_codes", [P, GROUPS, 2, W], U32)
-        taps_scales = kept("taps_scales", [P, GROUPS, 2, W], U8)
-        v_raw = kept("v_raw", [P, GROUPS, 2 * W], U8)
+        sample_codes = kept("sample_codes", [P, HALVES, CHUNKS, W], U32)
+        sample_scales = kept("sample_scales", [P, HALVES, CHUNKS, W], U8)
+        taps_raw = kept("taps_raw", [P, GROUPS, CORE_CHUNKS, PACK, W], BF16)
+        taps_codes = kept("taps_codes", [P, GROUPS, CORE_CHUNKS, W], U32)
+        taps_scales = kept("taps_scales", [P, GROUPS, CORE_CHUNKS, W], U8)
+        v_words_raw = kept("v_words_raw", [P, GROUPS, 2 * W], U8)
         v_words = kept("v_words", [P, GROUPS, 2 * W], U8)
         v_scales_raw = kept("v_scales_raw", [P, GROUPS, W], U8)
         v_scales = kept("v_scales", [P, GROUPS, W], U8)
-        c_words = kept("c_words", [P, GROUPS, 2 * W], U8)
-        c_scales = kept("c_scales", [P, GROUPS, W], U8)
+        c_words = kept("c_words", [P, GROUPS, 2 * BANDS], U8)
+        c_scales = kept("c_scales", [P, GROUPS, BANDS], U8)
         gain = kept("gain", [P, GROUPS, PACK], BF16)
         gain_sign = kept("gain_sign", [P, GROUPS * PACK], F32)
         gain_size = kept("gain_size", [P, GROUPS * PACK], F32)
         gain_root = kept("gain_root", [P, GROUPS * PACK], F32)
-        half = kept("half", [P, GROUPS * PACK], F32)
+        one_half = kept("one_half", [P, GROUPS * PACK], F32)
         ones = kept("ones", [P, P, PACK], BF16)
         ones_codes = kept("ones_codes", [P, P], U32)
         ones_scales = kept("ones_scales", [P, P], U8)
         level_rows = kept("level_rows", [P, BANDS], BF16)
-        e_codes = kept("e_codes", [P, HALVES, GROUPS, W], U32)
-        e_scales = kept("e_scales", [P, HALVES, GROUPS, W], U8)
+        energy_codes = kept("energy_codes", [P, HALVES, GROUPS, W], U32)
+        energy_scales = kept("energy_scales", [P, HALVES, GROUPS, W], U8)
         result = kept("result", [P, HALVES, PACK, BANDS], F32)
-        live = {}
-        free_banks = list(range(8))
+
+        free_banks = list(range(PSUM_BANKS))
+        banks = {}
+        staged = {}
 
         def take_bank(key, shape):
             number = free_banks[0]
             free_banks.remove(number)
-            live[key] = psum.tile(shape, F32, name="bank", tag="bank%d" % number)
-            live["number", key] = number
-            return live[key]
+            tile = psum.tile(shape, F32, name="bank", tag="bank%d" % number)
+            banks[key] = (number, tile)
+            return tile
 
         def give_bank(key):
-            free_banks.append(live["number", key])
-            return live[key]
+            number, tile = banks[key]
+            free_banks.append(number)
+            return tile
 
-        def copy_on(engine, out, in_):
+        def staging(kind, key, shape, bufs):
+            if (kind, key) not in staged:
+                staged[kind, key] = stage.tile(shape, BF16, name=kind, bufs=bufs, align_bytes=64)
+            return staged[kind, key]
+
+        def copy_on(engine, target, source):
             if engine == "scalar":
-                nc.scalar.copy(out=out, in_=in_)
+                nc.scalar.copy(out=target, in_=source)
             else:
-                nc.vector.tensor_copy(out=out, in_=in_)
+                nc.vector.tensor_copy(out=target, in_=source)
+
+        def quantize(codes, scales, grouped):
+            nc.vector.quantize_mx(out=codes.bitcast(FP8X4), scales=scales, in_=grouped.rearrange("p n t -> p (n t)"))
 
         def setup():
             nc.scalar.dma_start(out=gain[:], in_=whiten.rearrange("(g p t) -> p g t", p=P, t=PACK))
             nc.vector.memset(v_scales_raw[:].bitcast(I32), 0)
             nc.vector.memset(ones[:], 1.0)
-            nc.vector.memset(warm[:, 0:8], 0.0)
+            nc.vector.memset(table_probe[:, 0, :], 0.0)
             quantize(ones_codes[:], ones_scales[:], ones[:])
             nc.vector.memset(c_scales[:].bitcast(I32), 0)
             make_identity(nc, identity[:])
-            nc.scalar.activation(out=warm[:, 8:16], in_=warm[:, 0:8], func=ACT.Square)
-            flat = gain[:].rearrange("p g t -> p (g t)")
-            nc.gpsimd.memset(half[:], 0.5)
-            nc.scalar.activation(out=gain_size[:], in_=flat, func=ACT.Abs)
-            nc.scalar.activation(out=gain_sign[:], in_=flat, func=ACT.Sign)
-            nc.gpsimd.tensor_tensor(out=gain_root[:], in0=gain_size[:], in1=half[:], op=ALU.pow)
+            nc.scalar.activation(out=table_probe[:, 1, :], in_=table_probe[:, 0, :], func=ACT.Square)
+            gain_columns = gain[:].rearrange("p g t -> p (g t)")
+            nc.gpsimd.memset(one_half[:], 0.5)
+            nc.scalar.activation(out=gain_size[:], in_=gain_columns, func=ACT.Abs)
+            nc.scalar.activation(out=gain_sign[:], in_=gain_columns, func=ACT.Sign)
+            nc.gpsimd.tensor_tensor(out=gain_root[:], in0=gain_size[:], in1=one_half[:], op=ALU.pow)
 
         def warm_up(passes):
             bank = take_bank("warm", [P, P])
@@ -113,43 +140,38 @@ def tile_multitaper_band_sensing_s3_kernel(
                 )
             give_bank("warm")
 
-        def load_edge(h, i0, i1):
-            rows = edge[h * W : (h + 1) * W, :].rearrange("(r i) k -> r i k", i=PACK)
-            nc.sync.dma_start(out=edge_raw[:, h, i0:i1, :], in_=rows[:, i0:i1, :])
+        def load_frames(target, source, h, tiles):
+            rows = source[h * W : (h + 1) * W, :].rearrange("(r i) k -> r i k", i=PACK)
+            nc.sync.dma_start(out=target[:, h, tiles, :], in_=rows[:, tiles, :])
 
-        def load_core(h, i0, i1, c0, c1):
-            rows = core[h * W : (h + 1) * W, c0 * W : c1 * W].rearrange("(r i) k -> r i k", i=PACK)
-            nc.sync.dma_start(out=core_raw[:, h, i0:i1, c0 * W : c1 * W], in_=rows[:, i0:i1, :])
+        def load_taps(g, c):
+            rows = core_taps[c * W : (c + 1) * W, g * W : (g + 1) * W].rearrange("(p j) f -> p j f", j=PACK)
+            nc.sync.dma_start(out=taps_raw[:, g, c], in_=rows)
 
-        def load_taps(g0, g1, c):
-            rows = core_taps[c * W : (c + 1) * W, g0 * W : g1 * W].rearrange("(p j) f -> p j f", j=PACK)
-            nc.sync.dma_start(out=taps_raw[:, c, :, g0 * W : g1 * W], in_=rows)
-
-        def load_v_words(g0, g1):
-            words = edge_taps_words[0][:, 2 * W * g0 : 2 * W * g1]
-            target = v_raw[:, g0:g1].rearrange("p g n -> p (g n)")
+        def load_v_words(groups):
+            words = edge_taps_words[0][:, 2 * W * groups.start : 2 * W * groups.stop]
+            target = v_words_raw[:, groups].rearrange("p g n -> p (g n)")
             nc.sync.dma_start(out=target.bitcast(I32), in_=words.bitcast(I32))
 
         def load_v_scales():
             plane = v_scales_raw[:].rearrange("p g n -> p (g n)").bitcast(I32)
-            for q in range(4):
-                nc.sync.dma_start(out=plane[32 * q : 32 * q + 4, :], in_=edge_taps_scales[0][4 * q : 4 * q + 4, :].bitcast(I32))
+            for q in range(P // QUADRANT):
+                rows = edge_taps_scales[0][SCALE_ROWS * q : SCALE_ROWS * (q + 1), :]
+                nc.sync.dma_start(out=plane[QUADRANT * q : QUADRANT * q + SCALE_ROWS, :], in_=rows.bitcast(I32))
 
-        def load_combine_words():
+        def load_c_words():
             nc.sync.dma_start(out=c_words[:].bitcast(I32), in_=combine_words.rearrange("g p n -> p g n").bitcast(I32))
 
-        def load_combine_scales():
-            for q in range(4):
-                rows = combine_scales[:, 4 * q : 4 * q + 4, :].rearrange("g r n -> r g n")
-                nc.sync.dma_start(out=c_scales[32 * q : 32 * q + 4].bitcast(I32), in_=rows.bitcast(I32))
+        def load_c_scales():
+            for q in range(P // QUADRANT):
+                rows = combine_scales[:, SCALE_ROWS * q : SCALE_ROWS * (q + 1), :].rearrange("g r n -> r g n")
+                target = c_scales[QUADRANT * q : QUADRANT * q + SCALE_ROWS]
+                nc.sync.dma_start(out=target.bitcast(I32), in_=rows.bitcast(I32))
 
-        def load_level():
-            nc.sync.dma_start(out=level_rows[:], in_=level.partition_broadcast(P))
-
-        def order_v_words(g0, g1):
+        def order_v_words(groups):
             nc.vector.tensor_copy(
-                out=v_words[:, g0:g1].rearrange("p g (t m b) -> p g t m b", t=PACK, b=2),
-                in_=v_raw[:, g0:g1].rearrange("p g (m t b) -> p g t m b", t=PACK, b=2),
+                out=v_words[:, groups].rearrange("p g (t m b) -> p g t m b", t=PACK, b=2),
+                in_=v_words_raw[:, groups].rearrange("p g (m t b) -> p g t m b", t=PACK, b=2),
             )
 
         def order_v_scales():
@@ -159,40 +181,36 @@ def tile_multitaper_band_sensing_s3_kernel(
             )
 
         def transpose(h, s, pair):
-            turned = take_bank(("turned", h, s, pair), [P, 2, 2, P])
+            bank = take_bank(("turned", h, s, pair), [P, 2, 2, P])
             samples = edge_raw[:, h] if s == 0 else core_raw[:, h, :, (s - 1) * W : s * W]
             words = samples.bitcast(F32)
             for i in range(2):
                 for u in range(2):
-                    nc.tensor.transpose(turned[:, i, u, :], words[:, 2 * pair + i, u : 2 * P : 2], identity[:])
+                    nc.tensor.transpose(bank[:, i, u, :], words[:, 2 * pair + i, u : 2 * P : 2], identity[:])
 
         def unload(h, s, pair, engine):
-            if ("x", h, s) not in live:
-                live["x", h, s] = stage.tile([P, W, PACK], BF16, name="x_grouped", bufs=4, align_bytes=64)
-            words = live["x", h, s][:].rearrange("p n t -> p (n t)").bitcast(F32)[:, pair * W : (pair + 1) * W]
+            grouped = staging("samples_grouped", (h, s), [P, W, PACK], SAMPLE_BUFS)
+            words = grouped[:].rearrange("p n t -> p (n t)").bitcast(F32)[:, pair * W : (pair + 1) * W]
             copy_on(
                 engine,
                 words.rearrange("p (i r u) -> p i r u", i=2, u=2),
                 give_bank(("turned", h, s, pair))[:].rearrange("p i u r -> p i r u"),
             )
 
-        def quantize(codes, scales, grouped):
-            nc.vector.quantize_mx(out=codes.bitcast(FP8X4), scales=scales, in_=grouped.rearrange("p n t -> p (n t)"))
-
         def quantize_samples(h, s):
-            quantize(x_codes[:, h, s], x_scales[:, h, s], live["x", h, s][:])
+            quantize(sample_codes[:, h, s], sample_scales[:, h, s], staged["samples_grouped", (h, s)][:])
 
-        def group_taps(g, c, t0, t1, engine):
-            if ("taps", g, c) not in live:
-                live["taps", g, c] = stage.tile([P, W, PACK], BF16, name="taps_grouped", bufs=4, align_bytes=64)
+        def group_taps(g, c, columns, engine):
+            grouped = staging("taps_grouped", (g, c), [P, W, PACK], TAPS_BUFS)
+            tiles = slice(columns.start // P, columns.stop // P)
             copy_on(
                 engine,
-                live["taps", g, c][:].rearrange("p (t a b) j -> p t a j b", t=PACK, b=2)[:, t0:t1],
-                taps_raw[:, c, :, g * W : (g + 1) * W].rearrange("p j (a b t) -> p t a j b", t=PACK, b=2)[:, t0:t1],
+                grouped[:].rearrange("p (t a b) j -> p t a j b", t=PACK, b=2)[:, tiles],
+                taps_raw[:, g, c].rearrange("p j (a b t) -> p t a j b", t=PACK, b=2)[:, tiles],
             )
 
         def quantize_taps(g, c):
-            quantize(taps_codes[:, g, c], taps_scales[:, g, c], live["taps", g, c][:])
+            quantize(taps_codes[:, g, c], taps_scales[:, g, c], staged["taps_grouped", (g, c)][:])
 
         def filter_pass(h, g, t, s):
             if s == 0:
@@ -203,362 +221,239 @@ def tile_multitaper_band_sensing_s3_kernel(
                 codes = taps_codes[:, g, s - 1, P * t : P * (t + 1)].bitcast(FP8X4)
                 scales = taps_scales[:, g, s - 1, P * t : P * (t + 1)]
             nc.tensor.matmul_mx(
-                out=live["y", h, g, t][:],
+                out=banks["y", h, g, t][1][:],
                 lhsT=codes,
                 lhsT_scale=scales,
-                rhs=x_codes[:, h, s].bitcast(FP8X4),
-                rhs_scale=x_scales[:, h, s],
+                rhs=sample_codes[:, h, s].bitcast(FP8X4),
+                rhs_scale=sample_scales[:, h, s],
                 start=(s == 0),
                 stop=(s == CHUNKS - 1),
             )
+
+        def chunk_passes(h, g, s, tiles=range(PACK)):
+            for t in tiles:
+                filter_pass(h, g, t, s)
 
         def filter_tile(h, g, t):
             for s in range(CHUNKS):
                 filter_pass(h, g, t, s)
 
-        def square_scaled(h, g, t):
-            if ("squares", h, g) not in live:
-                live["squares", h, g] = stage.tile([P, PACK, W], BF16, name="squares", bufs=4)
-            column = PACK * g + t
-            nc.scalar.activation(
-                out=live["squares", h, g][:, t, :],
-                in_=give_bank(("y", h, g, t))[:],
-                func=ACT.Square,
-                scale=gain_root[:, column : column + 1],
-            )
+        def square(h, g, *tiles):
+            squares = staging("squares", (h, g), [P, PACK, W], SQUARE_BUFS)
+            for t in tiles:
+                column = PACK * g + t
+                nc.scalar.activation(
+                    out=squares[:, t, :],
+                    in_=give_bank(("y", h, g, t))[:],
+                    func=ACT.Square,
+                    scale=gain_root[:, column : column + 1],
+                )
 
-        def sign_energy(h, g, t):
-            column = PACK * g + t
-            rows = live["squares", h, g][:, t, :]
-            nc.vector.tensor_scalar(
-                out=rows, in0=rows, scalar1=gain_sign[:, column : column + 1], scalar2=None, op0=ALU.mult
-            )
+        def apply_sign(h, g):
+            for t in range(PACK):
+                column = PACK * g + t
+                rows = staged["squares", (h, g)][:, t, :]
+                nc.vector.tensor_scalar(
+                    out=rows, in0=rows, scalar1=gain_sign[:, column : column + 1], scalar2=None, op0=ALU.mult
+                )
 
-        def scale_energy(h, g, t):
-            if ("scaled", h, g) not in live:
-                live["scaled", h, g] = stage.tile([P, PACK, W], BF16, name="scaled", bufs=2)
-            column = PACK * g + t
-            nc.vector.tensor_scalar(
-                out=live["scaled", h, g][:, t, :],
-                in0=live["squares", h, g][:, t, :],
-                scalar1=gain[:].rearrange("p g t -> p (g t)")[:, column : column + 1],
-                scalar2=None,
-                op0=ALU.mult,
-            )
-
-        def group_energy(h, g, n0, n1, engine):
-            if ("e", h, g) not in live:
-                live["e", h, g] = stage.tile([P, W, PACK], BF16, name="e_grouped", align_bytes=64)
+        def group_energy(h, g, frames, engine):
+            grouped = staging("energy_grouped", (h, g), [P, W, PACK], ENERGY_BUFS)
             copy_on(
                 engine,
-                live["e", h, g][:, n0:n1, :].rearrange("p (a b) t -> p a t b", b=4),
-                live.get(("scaled", h, g), live["squares", h, g])[:, :, n0:n1].rearrange("p t (a b) -> p a t b", b=4),
+                grouped[:, frames, :].rearrange("p (a b) t -> p a t b", b=4),
+                staged["squares", (h, g)][:, :, frames].rearrange("p t (a b) -> p a t b", b=4),
             )
 
-        def square(h, g, t):
-            if ("squares", h, g) not in live:
-                live["squares", h, g] = stage.tile([P, PACK, W], F32, name="squares", bufs=4)
-            nc.scalar.activation(out=live["squares", h, g][:, t, :], in_=give_bank(("y", h, g, t))[:], func=ACT.Square)
-
-        def whiten_energy(h, g, n0, n1):
-            if ("e", h, g) not in live:
-                live["e", h, g] = stage.tile([P, W, PACK], BF16, name="e_grouped", align_bytes=64)
-            nc.vector.tensor_tensor(
-                out=live["e", h, g][:, n0:n1, :].rearrange("p (a b) t -> p a t b", b=2),
-                in0=live["squares", h, g][:, :, n0:n1].rearrange("p t (a b) -> p a t b", b=2),
-                in1=gain[:, g, :].unsqueeze(1).unsqueeze(3).to_broadcast([P, (n1 - n0) // 2, PACK, 2]),
-                op=ALU.mult,
-            )
-
-        def filter_narrow(h, g, i):
-            bank = take_bank(("y4", h, g, i), [P, PACK, P])
-            frames = slice(P * i, P * (i + 1))
-            for t in range(PACK):
-                for s in range(CHUNKS):
-                    if s == 0:
-                        codes = v_words[:, g, 2 * P * t : 2 * P * (t + 1)].bitcast(FP4X4)
-                        scales = v_scales[:, g, P * t : P * (t + 1)]
-                    else:
-                        codes = taps_codes[:, g, s - 1, P * t : P * (t + 1)].bitcast(FP8X4)
-                        scales = taps_scales[:, g, s - 1, P * t : P * (t + 1)]
-                    nc.tensor.matmul_mx(
-                        out=bank[:, t, :],
-                        lhsT=codes,
-                        lhsT_scale=scales,
-                        rhs=x_codes[:, h, s, frames].bitcast(FP8X4),
-                        rhs_scale=x_scales[:, h, s, frames],
-                        start=(s == 0),
-                        stop=(s == CHUNKS - 1),
-                    )
-
-        def square_narrow(h, g, i):
-            if ("squares", h, g) not in live:
-                live["squares", h, g] = stage.tile([P, W, PACK], F32, name="squares", bufs=4)
-            nc.scalar.activation(
-                out=live["squares", h, g][:, P * i : P * (i + 1), :],
-                in_=give_bank(("y4", h, g, i))[:].rearrange("p t n -> p n t"),
-                func=ACT.Square,
-            )
-
-        def whiten_narrow(h, g, i):
-            if ("e", h, g) not in live:
-                live["e", h, g] = stage.tile([P, W, PACK], BF16, name="e_grouped", align_bytes=64)
-            nc.vector.tensor_tensor(
-                out=live["e", h, g][:, P * i : P * (i + 1), :],
-                in0=live["squares", h, g][:, P * i : P * (i + 1), :],
-                in1=gain[:, g, :].unsqueeze(1).to_broadcast([P, P, PACK]),
-                op=ALU.mult,
-            )
-
-        def quantize_energy(h, g, n0, n1):
-            quantize(e_codes[:, h, g, n0:n1], e_scales[:, h, g, n0:n1], live["e", h, g][:, n0:n1, :])
+        def quantize_energy(h, g, frames):
+            grouped = staged["energy_grouped", (h, g)]
+            quantize(energy_codes[:, h, g, frames], energy_scales[:, h, g, frames], grouped[:, frames, :])
 
         def band_pass(h, i, g):
             if g == 0:
                 take_bank(("z", h, i), [P, BANDS])
             nc.tensor.matmul_mx(
-                out=live["z", h, i][:],
-                lhsT=e_codes[:, h, g, P * i : P * (i + 1)].bitcast(FP8X4),
-                lhsT_scale=e_scales[:, h, g, P * i : P * (i + 1)],
+                out=banks["z", h, i][1][:],
+                lhsT=energy_codes[:, h, g, P * i : P * (i + 1)].bitcast(FP8X4),
+                lhsT_scale=energy_scales[:, h, g, P * i : P * (i + 1)],
                 rhs=c_words[:, g].bitcast(FP4X4),
                 rhs_scale=c_scales[:, g],
                 start=(g == 0),
                 stop=(g == GROUPS - 1),
             )
 
-        def subtract_level(h, i, n0, n1):
-            bank = give_bank(("z", h, i)) if n1 == BANDS else live["z", h, i]
-            nc.vector.tensor_tensor(
-                out=result[:, h, i, n0:n1], in0=bank[:, n0:n1], in1=level_rows[:, n0:n1], op=ALU.subtract
-            )
+        def band_passes(*steps):
+            for h, i, g in steps:
+                band_pass(h, i, g)
 
-        def store(h, i, n0, n1):
+        def finish(h, i, bands=ALL):
+            bank = give_bank(("z", h, i)) if bands.stop == BANDS else banks["z", h, i][1]
+            nc.vector.tensor_tensor(
+                out=result[:, h, i, bands], in0=bank[:, bands], in1=level_rows[:, bands], op=ALU.subtract
+            )
             rows = out[h * W : (h + 1) * W, :].rearrange("(r i) b -> r i b", i=PACK)
-            nc.sync.dma_start(out=rows[:, i, n0:n1], in_=result[:, h, i, n0:n1])
+            nc.sync.dma_start(out=rows[:, i, bands], in_=result[:, h, i, bands])
 
         setup()
-        load_v_words(0, 1)
-        warm_up(4)
-        warm_up(4)
-        warm_up(4)
-        load_edge(1, 0, 4)
-        warm_up(4)
-        load_edge(0, 0, 2)
-        transpose(1, 0, 1)
-        unload(1, 0, 1, "vector")
-        load_edge(0, 2, 4)
-        transpose(1, 0, 0)
-        unload(1, 0, 0, "scalar")
-        warm_up(4)
+
+        first_pair, second_pair, all_tiles = slice(0, 2), slice(2, PACK), slice(0, PACK)
+        first_group, later_groups = slice(0, 1), slice(1, GROUPS)
+        load_frames(edge_raw, edge, 0, first_pair)
+        load_frames(edge_raw, edge, 0, second_pair)
+        load_frames(core_raw, core, 0, first_pair)
+        load_frames(core_raw, core, 0, second_pair)
         load_v_scales()
-        warm_up(4)
+        load_frames(edge_raw, edge, 1, all_tiles)
+        load_v_words(first_group)
+        load_taps(0, 0)
+        load_frames(core_raw, core, 1, first_pair)
+        load_v_words(later_groups)
+        load_taps(0, 1)
+        load_frames(core_raw, core, 1, second_pair)
+        load_taps(1, 0)
+        load_taps(1, 1)
+        load_c_scales()
+        load_taps(2, 0)
+        load_taps(2, 1)
+        load_c_words()
+        nc.sync.dma_start(out=level_rows[:], in_=level.partition_broadcast(P))
+
+
+        warm_up(WARM_PASSES_AT_START)
         transpose(0, 0, 0)
         unload(0, 0, 0, "scalar")
-        order_v_words(0, 1)
-        load_core(0, 0, 2, 0, 2)
-        warm_up(4)
         transpose(0, 0, 1)
-        load_core(0, 2, 4, 0, 2)
-        unload(0, 0, 1, "scalar")
-        load_taps(0, 1, 0)
+        unload(0, 0, 1, "vector")
         transpose(0, 1, 0)
-        quantize_samples(1, 0)
         unload(0, 1, 0, "scalar")
-        load_core(1, 2, 4, 0, 2)
+        warm_up(WARM_PASSES_BETWEEN_LOADS)
+        quantize_samples(0, 0)
         order_v_scales()
         transpose(0, 1, 1)
-        quantize_samples(0, 0)
-        group_taps(0, 0, 0, 2, "vector")
         unload(0, 1, 1, "scalar")
-        quantize_samples(0, 1)
-        transpose(0, 2, 1)
-        filter_pass(1, 0, 1, 0)
-        filter_pass(1, 0, 3, 0)
         transpose(0, 2, 0)
-        unload(0, 2, 1, "vector")
-        group_taps(0, 0, 2, 4, "scalar")
-        load_taps(0, 1, 1)
-        filter_pass(1, 0, 0, 0)
         unload(0, 2, 0, "scalar")
-        filter_pass(0, 0, 3, 0)
-        load_core(1, 0, 2, 0, 2)
-        quantize_taps(0, 0)
-        group_taps(0, 1, 2, 4, "vector")
-        load_v_words(1, 3)
+        transpose(0, 2, 1)
+        unload(0, 2, 1, "scalar")
+        order_v_words(first_group)
+        quantize_samples(0, 1)
+        transpose(1, 0, 0)
+        transpose(1, 0, 1)
+
+        group_taps(0, 0, FIRST, "scalar")
+        group_taps(0, 0, SECOND, "vector")
         quantize_samples(0, 2)
-        transpose(1, 2, 1)
-        group_taps(0, 1, 0, 2, "scalar")
-        quantize_taps(0, 1)
-        unload(1, 2, 1, "scalar")
-        order_v_words(1, 3)
-        transpose(1, 1, 1)
-        load_taps(1, 2, 0)
-        unload(1, 1, 1, "scalar")
-        filter_pass(0, 0, 2, 0)
-        filter_pass(0, 0, 2, 1)
-        transpose(1, 2, 0)
+        chunk_passes(0, 0, 0)
+        unload(1, 0, 0, "scalar")
+        unload(1, 0, 1, "scalar")
         transpose(1, 1, 0)
-        unload(1, 2, 0, "scalar")
-        quantize_samples(1, 2)
-        filter_pass(0, 0, 1, 0)
+        transpose(1, 2, 0)
+        quantize_taps(0, 0)
+        order_v_words(later_groups)
         unload(1, 1, 0, "scalar")
-        group_taps(1, 0, 2, 4, "scalar")
-        filter_pass(0, 0, 3, 1)
-        filter_pass(0, 0, 3, 2)
-        load_taps(1, 2, 1)
-        group_taps(1, 1, 2, 4, "scalar")
+        group_taps(0, 1, SECOND, "scalar")
+        group_taps(0, 1, FIRST, "vector")
+        quantize_samples(1, 0)
+        chunk_passes(0, 0, 1)
+        unload(1, 2, 0, "scalar")
+        transpose(1, 1, 1)
+        transpose(1, 2, 1)
+        quantize_taps(0, 1)
+        unload(1, 1, 1, "scalar")
+        unload(1, 2, 1, "scalar")
+
+        chunk_passes(1, 0, 0, tiles=(0, 1))
+        chunk_passes(0, 0, 2)
+        group_taps(1, 0, FIRST, "vector")
         quantize_samples(1, 1)
-        load_taps(2, 3, 0)
-        filter_pass(0, 0, 1, 1)
-        filter_pass(1, 0, 2, 0)
-        filter_pass(0, 0, 0, 0)
-        filter_pass(0, 0, 0, 1)
-        filter_pass(0, 0, 0, 2)
-        filter_pass(1, 0, 3, 1)
-        group_taps(1, 0, 0, 2, "vector")
-        filter_pass(1, 0, 3, 2)
-        filter_pass(0, 0, 1, 2)
-        square_scaled(1, 0, 3)
-        group_taps(1, 1, 0, 2, "vector")
-        load_taps(2, 3, 1)
+        quantize_samples(1, 2)
+        group_taps(1, 0, SECOND, "scalar")
+        group_taps(1, 1, FIRST, "vector")
+        group_taps(1, 1, SECOND, "scalar")
         quantize_taps(1, 0)
         quantize_taps(1, 1)
-        sign_energy(1, 0, 3)
-        filter_pass(1, 0, 1, 1)
-        group_taps(2, 0, 2, 4, "vector")
-        load_combine_scales()
-        group_taps(2, 0, 0, 2, "vector")
-        filter_pass(0, 0, 2, 2)
-        square_scaled(0, 0, 2)
-        sign_energy(0, 0, 2)
-        filter_pass(1, 0, 1, 2)
-        filter_pass(1, 0, 2, 1)
-        filter_pass(1, 0, 0, 1)
-        filter_pass(1, 0, 2, 2)
-        group_taps(2, 1, 2, 4, "vector")
-        group_taps(2, 1, 0, 2, "vector")
-        filter_pass(1, 0, 0, 2)
-        filter_tile(0, 1, 3)
-        filter_tile(0, 1, 1)
-        quantize_taps(2, 0)
-        square_scaled(1, 0, 1)
-        square_scaled(0, 0, 1)
-        quantize_taps(2, 1)
-        sign_energy(0, 0, 1)
-        load_level()
-        square_scaled(1, 0, 2)
-        square_scaled(1, 0, 0)
-        filter_tile(0, 1, 2)
-        load_combine_words()
+        square(0, 0, 0, 1)
+        chunk_passes(1, 0, 0, tiles=(2, 3))
+        chunk_passes(1, 0, 1)
+        chunk_passes(1, 0, 2)
+        square(0, 0, 2, 3)
+
+        group_taps(2, 0, ALL, "vector")
+        group_taps(2, 1, ALL, "vector")
         filter_tile(0, 1, 0)
-        square_scaled(0, 0, 3)
-        sign_energy(1, 0, 2)
+        square(1, 0, 0, 1)
+        filter_tile(0, 1, 1)
+        square(1, 0, 2, 3)
+        filter_tile(0, 1, 2)
+        quantize_taps(2, 0)
+        quantize_taps(2, 1)
+        apply_sign(0, 0)
+        apply_sign(1, 0)
+        filter_tile(0, 1, 3)
+        square(0, 1, 0, 1)
         filter_tile(1, 1, 0)
-        filter_tile(0, 2, 3)
-        square_scaled(0, 1, 1)
-        sign_energy(1, 0, 0)
-        sign_energy(0, 0, 3)
-        square_scaled(0, 0, 0)
+        square(0, 1, 2, 3)
+        group_energy(0, 0, ALL, "vector")
+        group_energy(1, 0, ALL, "vector")
+
         filter_tile(0, 2, 0)
-        square_scaled(0, 1, 2)
-        sign_energy(1, 0, 1)
         filter_tile(0, 2, 1)
-        square_scaled(0, 1, 3)
-        square_scaled(0, 1, 0)
+        square(0, 2, 0)
         filter_tile(0, 2, 2)
-        sign_energy(0, 0, 0)
-        sign_energy(0, 1, 1)
-        sign_energy(0, 1, 2)
-        square_scaled(0, 2, 3)
-        group_energy(1, 0, 0, 512, "vector")
-        sign_energy(0, 1, 3)
-        sign_energy(0, 1, 0)
-        quantize_energy(1, 0, 0, 512)
-        group_energy(0, 0, 0, 512, "vector")
-        filter_tile(1, 1, 3)
-        filter_tile(1, 2, 2)
-        sign_energy(0, 2, 3)
-        square_scaled(0, 2, 0)
-        sign_energy(0, 2, 0)
-        square_scaled(0, 2, 1)
-        sign_energy(0, 2, 1)
-        square_scaled(1, 1, 0)
-        sign_energy(1, 1, 0)
-        square_scaled(0, 2, 2)
-        sign_energy(0, 2, 2)
+        square(0, 2, 1)
+        filter_tile(0, 2, 3)
+        square(0, 2, 2)
+        apply_sign(0, 1)
+        quantize_energy(0, 0, ALL)
+        group_energy(0, 1, ALL, "vector")
         filter_tile(1, 1, 1)
-        square_scaled(1, 1, 3)
-        group_energy(0, 1, 0, 512, "vector")
-        sign_energy(1, 1, 3)
-        group_energy(0, 2, 0, 256, "vector")
-        square_scaled(1, 2, 2)
-        sign_energy(1, 2, 2)
-        group_energy(0, 2, 256, 512, "scalar")
+        square(0, 2, 3)
+        square(1, 1, 0)
         filter_tile(1, 1, 2)
+        square(1, 1, 1)
+        apply_sign(0, 2)
+        filter_tile(1, 1, 3)
+        square(1, 1, 2)
+        quantize_energy(0, 1, ALL)
+        quantize_energy(1, 0, ALL)
         filter_tile(1, 2, 0)
-        square_scaled(1, 1, 1)
-        quantize_energy(0, 0, 0, 512)
-        square_scaled(1, 1, 2)
-        filter_tile(1, 2, 3)
-        square_scaled(1, 2, 0)
+        square(1, 1, 3)
+        group_energy(0, 2, SECOND, "scalar")
+        apply_sign(1, 1)
         filter_tile(1, 2, 1)
-        band_pass(0, 0, 0)
-        sign_energy(1, 1, 1)
-        band_pass(1, 0, 0)
-        quantize_energy(0, 1, 0, 512)
-        quantize_energy(0, 2, 0, 256)
-        sign_energy(1, 1, 2)
-        quantize_energy(0, 2, 256, 512)
-        sign_energy(1, 2, 0)
-        square_scaled(1, 2, 3)
-        band_pass(0, 2, 0)
-        band_pass(0, 2, 1)
-        square_scaled(1, 2, 1)
-        band_pass(0, 2, 2)
-        group_energy(1, 1, 0, 256, "vector")
-        sign_energy(1, 2, 3)
-        sign_energy(1, 2, 1)
-        group_energy(1, 1, 256, 512, "scalar")
-        quantize_energy(1, 1, 0, 256)
-        subtract_level(0, 2, 0, 512)
-        store(0, 2, 0, 512)
-        band_pass(0, 3, 0)
-        band_pass(0, 3, 1)
-        band_pass(0, 3, 2)
-        group_energy(1, 2, 0, 256, "scalar")
-        group_energy(1, 2, 256, 512, "scalar")
-        subtract_level(0, 3, 0, 512)
-        band_pass(0, 0, 1)
-        band_pass(0, 0, 2)
-        subtract_level(0, 0, 0, 512)
-        band_pass(0, 1, 0)
-        band_pass(0, 1, 1)
+        square(1, 2, 0)
+        quantize_energy(0, 2, SECOND)
+        group_energy(0, 2, FIRST, "vector")
+        group_energy(1, 1, FIRST, "vector")
+        filter_tile(1, 2, 2)
+        square(1, 2, 1)
+        filter_tile(1, 2, 3)
+        square(1, 2, 2, 3)
+        quantize_energy(0, 2, FIRST)
+        quantize_energy(1, 1, FIRST)
+        apply_sign(1, 2)
+        group_energy(1, 1, SECOND, "scalar")
+        group_energy(1, 2, FIRST, "scalar")
+        group_energy(1, 2, SECOND, "scalar")
+
+        band_passes((0, 0, 0), (0, 1, 0), (0, 2, 0), (0, 0, 1), (0, 1, 1), (0, 2, 1), (0, 0, 2))
+        finish(0, 0)
         band_pass(0, 1, 2)
-        band_pass(1, 3, 0)
-        store(0, 3, 0, 512)
-        store(0, 0, 0, 512)
-        quantize_energy(1, 2, 0, 256)
-        subtract_level(0, 1, 0, 512)
-        quantize_energy(1, 1, 256, 512)
-        band_pass(1, 0, 1)
+        finish(0, 1)
+        band_passes((0, 3, 0), (0, 3, 1), (1, 0, 0), (0, 2, 2))
+        quantize_energy(1, 1, SECOND)
+        finish(0, 2)
+        band_pass(0, 3, 2)
+        quantize_energy(1, 2, FIRST)
+        finish(0, 3)
+        band_passes((1, 1, 0), (1, 2, 0), (1, 0, 1), (1, 1, 1), (1, 3, 0))
+        quantize_energy(1, 2, SECOND)
         band_pass(1, 0, 2)
-        subtract_level(1, 0, 0, 512)
-        store(0, 1, 0, 512)
-        quantize_energy(1, 2, 256, 512)
-        band_pass(1, 1, 0)
-        store(1, 0, 0, 512)
-        band_pass(1, 1, 1)
+        finish(1, 0)
         band_pass(1, 1, 2)
-        subtract_level(1, 1, 0, 512)
-        band_pass(1, 3, 1)
-        band_pass(1, 2, 0)
-        store(1, 1, 0, 512)
+        finish(1, 1)
+        band_passes((1, 2, 1), (1, 3, 1), (1, 2, 2))
+        finish(1, 2)
         band_pass(1, 3, 2)
-        subtract_level(1, 3, 256, 512)
-        store(1, 3, 256, 512)
-        subtract_level(1, 3, 0, 256)
-        store(1, 3, 0, 256)
-        band_pass(1, 2, 1)
-        band_pass(1, 2, 2)
-        subtract_level(1, 2, 0, 512)
-        store(1, 2, 0, 512)
+        finish(1, 3, FIRST)
+        finish(1, 3, SECOND)

@@ -26,6 +26,8 @@ CHUNKS = 1 + CORE_CHUNKS
 PSUM_BANKS = 8
 QUADRANT = 32
 SCALE_ROWS = 4
+TWO_BF16_ONES = 0x3F803F80
+ALIGN = 256
 
 ALL = slice(0, W)
 FIRST = slice(0, W // 2)
@@ -51,7 +53,7 @@ def tile_multitaper_band_sensing_s3_kernel(
         ctx.enter_context(tc.manual_schedule())
 
         def kept(name, shape, dtype):
-            return keep.tile(shape, dtype, name=name, align_bytes=64)
+            return keep.tile(shape, dtype, name=name, align_bytes=ALIGN)
 
         identity = kept("identity", [P, P], F32)
         table_probe = kept("table_probe", [P, 2, 8], F32)
@@ -99,7 +101,7 @@ def tile_multitaper_band_sensing_s3_kernel(
 
         def staging(kind, key, shape, bufs):
             if (kind, key) not in staged:
-                staged[kind, key] = stage.tile(shape, BF16, name=kind, bufs=bufs, align_bytes=64)
+                staged[kind, key] = stage.tile(shape, BF16, name=kind, bufs=bufs, align_bytes=ALIGN)
             return staged[kind, key]
 
         def copy_on(engine, target, source):
@@ -113,10 +115,10 @@ def tile_multitaper_band_sensing_s3_kernel(
 
         def setup():
             nc.scalar.dma_start(out=gain[:], in_=whiten.rearrange("(g p t) -> p g t", p=P, t=PACK))
-            nc.vector.memset(v_scales_raw[:].bitcast(I32), 0)
-            nc.vector.memset(ones[:], 1.0)
             nc.vector.memset(table_probe[:, 0, :], 0.0)
+            nc.vector.memset(ones[:].bitcast(U32), TWO_BF16_ONES)
             quantize(ones_codes[:], ones_scales[:], ones[:])
+            nc.vector.memset(v_scales_raw[:].bitcast(I32), 0)
             nc.vector.memset(c_scales[:].bitcast(I32), 0)
             make_identity(nc, identity[:])
             nc.scalar.activation(out=table_probe[:, 1, :], in_=table_probe[:, 0, :], func=ACT.Square)
@@ -298,13 +300,13 @@ def tile_multitaper_band_sensing_s3_kernel(
 
         first_pair, second_pair, all_tiles = slice(0, 2), slice(2, PACK), slice(0, PACK)
         first_group, later_groups = slice(0, 1), slice(1, GROUPS)
+        load_v_words(first_group)
         load_frames(edge_raw, edge, 0, first_pair)
         load_frames(edge_raw, edge, 0, second_pair)
         load_frames(core_raw, core, 0, first_pair)
-        load_frames(core_raw, core, 0, second_pair)
         load_v_scales()
+        load_frames(core_raw, core, 0, second_pair)
         load_frames(edge_raw, edge, 1, all_tiles)
-        load_v_words(first_group)
         load_taps(0, 0)
         load_frames(core_raw, core, 1, first_pair)
         load_v_words(later_groups)
@@ -312,9 +314,9 @@ def tile_multitaper_band_sensing_s3_kernel(
         load_frames(core_raw, core, 1, second_pair)
         load_taps(1, 0)
         load_taps(1, 1)
-        load_c_scales()
         load_taps(2, 0)
         load_taps(2, 1)
+        load_c_scales()
         load_c_words()
         nc.sync.dma_start(out=level_rows[:], in_=level.partition_broadcast(P))
 
@@ -323,26 +325,26 @@ def tile_multitaper_band_sensing_s3_kernel(
         transpose(0, 0, 0)
         unload(0, 0, 0, "scalar")
         transpose(0, 0, 1)
-        unload(0, 0, 1, "vector")
+        unload(0, 0, 1, "scalar")
         transpose(0, 1, 0)
         unload(0, 1, 0, "scalar")
         warm_up(WARM_PASSES_BETWEEN_LOADS)
+        order_v_words(first_group)
         quantize_samples(0, 0)
         order_v_scales()
-        transpose(0, 1, 1)
-        unload(0, 1, 1, "scalar")
         transpose(0, 2, 0)
         unload(0, 2, 0, "scalar")
         transpose(0, 2, 1)
         unload(0, 2, 1, "scalar")
-        order_v_words(first_group)
-        quantize_samples(0, 1)
+        transpose(0, 1, 1)
+        unload(0, 1, 1, "scalar")
+        quantize_samples(0, 2)
         transpose(1, 0, 0)
         transpose(1, 0, 1)
 
         group_taps(0, 0, FIRST, "scalar")
         group_taps(0, 0, SECOND, "vector")
-        quantize_samples(0, 2)
+        quantize_samples(0, 1)
         chunk_passes(0, 0, 0)
         unload(1, 0, 0, "scalar")
         unload(1, 0, 1, "scalar")
@@ -351,11 +353,11 @@ def tile_multitaper_band_sensing_s3_kernel(
         quantize_taps(0, 0)
         order_v_words(later_groups)
         unload(1, 1, 0, "scalar")
+        unload(1, 2, 0, "scalar")
         group_taps(0, 1, SECOND, "scalar")
         group_taps(0, 1, FIRST, "vector")
         quantize_samples(1, 0)
         chunk_passes(0, 0, 1)
-        unload(1, 2, 0, "scalar")
         transpose(1, 1, 1)
         transpose(1, 2, 1)
         quantize_taps(0, 1)
@@ -384,51 +386,52 @@ def tile_multitaper_band_sensing_s3_kernel(
         square(1, 0, 0, 1)
         filter_tile(0, 1, 1)
         square(1, 0, 2, 3)
-        filter_tile(0, 1, 2)
+        filter_tile(1, 1, 0)
         quantize_taps(2, 0)
         quantize_taps(2, 1)
         apply_sign(0, 0)
         apply_sign(1, 0)
-        filter_tile(0, 1, 3)
+        filter_tile(0, 1, 2)
         square(0, 1, 0, 1)
-        filter_tile(1, 1, 0)
-        square(0, 1, 2, 3)
+        filter_tile(0, 1, 3)
+        square(1, 1, 0)
+        square(0, 1, 2)
         group_energy(0, 0, ALL, "vector")
         group_energy(1, 0, ALL, "vector")
 
         filter_tile(0, 2, 0)
+        square(0, 1, 3)
         filter_tile(0, 2, 1)
         square(0, 2, 0)
         filter_tile(0, 2, 2)
         square(0, 2, 1)
         filter_tile(0, 2, 3)
         square(0, 2, 2)
-        apply_sign(0, 1)
         quantize_energy(0, 0, ALL)
-        group_energy(0, 1, ALL, "vector")
+        apply_sign(0, 1)
+        quantize_energy(1, 0, ALL)
         filter_tile(1, 1, 1)
         square(0, 2, 3)
-        square(1, 1, 0)
+        apply_sign(0, 2)
         filter_tile(1, 1, 2)
         square(1, 1, 1)
-        apply_sign(0, 2)
+        group_energy(0, 1, ALL, "vector")
         filter_tile(1, 1, 3)
         square(1, 1, 2)
-        quantize_energy(0, 1, ALL)
-        quantize_energy(1, 0, ALL)
+        group_energy(0, 2, FIRST, "vector")
         filter_tile(1, 2, 0)
         square(1, 1, 3)
         group_energy(0, 2, SECOND, "scalar")
         apply_sign(1, 1)
         filter_tile(1, 2, 1)
         square(1, 2, 0)
-        quantize_energy(0, 2, SECOND)
-        group_energy(0, 2, FIRST, "vector")
+        quantize_energy(0, 1, ALL)
         group_energy(1, 1, FIRST, "vector")
         filter_tile(1, 2, 2)
         square(1, 2, 1)
         filter_tile(1, 2, 3)
         square(1, 2, 2, 3)
+        quantize_energy(0, 2, SECOND)
         quantize_energy(0, 2, FIRST)
         quantize_energy(1, 1, FIRST)
         apply_sign(1, 2)
@@ -436,24 +439,23 @@ def tile_multitaper_band_sensing_s3_kernel(
         group_energy(1, 2, FIRST, "scalar")
         group_energy(1, 2, SECOND, "scalar")
 
-        band_passes((0, 0, 0), (0, 1, 0), (0, 2, 0), (0, 0, 1), (0, 1, 1), (0, 2, 1), (0, 0, 2))
+        band_passes((0, 0, 0), (0, 0, 1), (0, 1, 0), (0, 1, 1), (0, 2, 0), (0, 0, 2))
         finish(0, 0)
         band_pass(0, 1, 2)
-        finish(0, 1)
-        band_passes((0, 3, 0), (0, 3, 1), (1, 0, 0), (0, 2, 2))
         quantize_energy(1, 1, SECOND)
+        finish(0, 1)
+        band_passes((0, 2, 1), (0, 2, 2))
         finish(0, 2)
-        band_pass(0, 3, 2)
+        band_passes((1, 0, 0), (0, 3, 0), (0, 3, 1), (0, 3, 2))
         quantize_energy(1, 2, FIRST)
         finish(0, 3)
-        band_passes((1, 1, 0), (1, 2, 0), (1, 0, 1), (1, 1, 1), (1, 3, 0))
+        band_passes((1, 0, 1), (1, 1, 0), (1, 1, 1), (1, 0, 2))
         quantize_energy(1, 2, SECOND)
-        band_pass(1, 0, 2)
         finish(1, 0)
         band_pass(1, 1, 2)
         finish(1, 1)
-        band_passes((1, 2, 1), (1, 3, 1), (1, 2, 2))
+        band_passes((1, 2, 0), (1, 2, 1), (1, 2, 2))
         finish(1, 2)
-        band_pass(1, 3, 2)
+        band_passes((1, 3, 0), (1, 3, 1), (1, 3, 2))
         finish(1, 3, FIRST)
         finish(1, 3, SECOND)

from contextlib import ExitStack

import concourse.mybir as mybir
from concourse.masks import make_identity

FRAMES, CORE, EDGE, FILTERS, BANDS = 1024, 1024, 512, 1536, 512
FLOPS = 2 * FRAMES * (CORE + EDGE) * FILTERS + 2 * FRAMES * FILTERS * BANDS

F32 = mybir.dt.float32
BF16 = mybir.dt.bfloat16
I32 = mybir.dt.int32
U32 = mybir.dt.uint32
U8 = mybir.dt.uint8
FP8X4 = mybir.dt.float8_e4m3fn_x4
FP4X4 = mybir.dt.float4_e2m1fn_x4
ALU = mybir.AluOpType
ACT = mybir.ActivationFunctionType

P = 128
PACK = 4
W = P * PACK
HALVES = FRAMES // W
GROUPS = FILTERS // W
CORE_CHUNKS = CORE // W
CHUNKS = 1 + CORE_CHUNKS
PSUM_BANKS = 8
QUADRANT = 32
SCALE_ROWS = 4
TWO_BF16_ONES = 0x3F803F80
ALIGN = 256

ALL = slice(0, W)
FIRST = slice(0, W // 2)
SECOND = slice(W // 2, W)

SAMPLE_BUFS = 4
TAPS_BUFS = 4
SQUARE_BUFS = 4
ENERGY_BUFS = 3

WARM_PASSES_AT_START = 16
WARM_PASSES_BETWEEN_LOADS = 8


def tile_multitaper_band_sensing_s3_kernel(
    tc, core, edge, core_taps, edge_taps_words, edge_taps_scales, whiten, combine_words, combine_scales, level, out
):
    nc = tc.nc
    with ExitStack() as ctx:
        keep = ctx.enter_context(tc.tile_pool(name="keep", bufs=1))
        stage = ctx.enter_context(tc.tile_pool(name="stage", bufs=1))
        psum = ctx.enter_context(tc.psum_pool(name="psum", bufs=1))
        ctx.enter_context(tc.manual_schedule())

        def kept(name, shape, dtype):
            return keep.tile(shape, dtype, name=name, align_bytes=ALIGN)

        identity = kept("identity", [P, P], F32)
        table_probe = kept("table_probe", [P, 2, 8], F32)
        edge_raw = kept("edge_raw", [P, HALVES, PACK, EDGE], BF16)
        core_raw = kept("core_raw", [P, HALVES, PACK, CORE], BF16)
        sample_codes = kept("sample_codes", [P, HALVES, CHUNKS, W], U32)
        sample_scales = kept("sample_scales", [P, HALVES, CHUNKS, W], U8)
        taps_raw = kept("taps_raw", [P, GROUPS, CORE_CHUNKS, PACK, W], BF16)
        taps_codes = kept("taps_codes", [P, GROUPS, CORE_CHUNKS, W], U32)
        taps_scales = kept("taps_scales", [P, GROUPS, CORE_CHUNKS, W], U8)
        v_words_raw = kept("v_words_raw", [P, GROUPS, 2 * W], U8)
        v_words = kept("v_words", [P, GROUPS, 2 * W], U8)
        v_scales_raw = kept("v_scales_raw", [P, GROUPS, W], U8)
        v_scales = kept("v_scales", [P, GROUPS, W], U8)
        c_words = kept("c_words", [P, GROUPS, 2 * BANDS], U8)
        c_scales = kept("c_scales", [P, GROUPS, BANDS], U8)
        gain = kept("gain", [P, GROUPS, PACK], BF16)
        gain_sign = kept("gain_sign", [P, GROUPS * PACK], F32)
        gain_size = kept("gain_size", [P, GROUPS * PACK], F32)
        gain_root = kept("gain_root", [P, GROUPS * PACK], F32)
        one_half = kept("one_half", [P, GROUPS * PACK], F32)
        ones = kept("ones", [P, P, PACK], BF16)
        ones_codes = kept("ones_codes", [P, P], U32)
        ones_scales = kept("ones_scales", [P, P], U8)
        level_rows = kept("level_rows", [P, BANDS], BF16)
        energy_codes = kept("energy_codes", [P, HALVES, GROUPS, W], U32)
        energy_scales = kept("energy_scales", [P, HALVES, GROUPS, W], U8)
        result = kept("result", [P, HALVES, PACK, BANDS], F32)

        free_banks = list(range(PSUM_BANKS))
        banks = {}
        staged = {}

        def take_bank(key, shape):
            number = free_banks[0]
            free_banks.remove(number)
            tile = psum.tile(shape, F32, name="bank", tag="bank%d" % number)
            banks[key] = (number, tile)
            return tile

        def give_bank(key):
            number, tile = banks[key]
            free_banks.append(number)
            return tile

        def staging(kind, key, shape, bufs):
            if (kind, key) not in staged:
                staged[kind, key] = stage.tile(shape, BF16, name=kind, bufs=bufs, align_bytes=ALIGN)
            return staged[kind, key]

        def copy_on(engine, target, source):
            if engine == "scalar":
                nc.scalar.copy(out=target, in_=source)
            else:
                nc.vector.tensor_copy(out=target, in_=source)

        def quantize(codes, scales, grouped):
            nc.vector.quantize_mx(out=codes.bitcast(FP8X4), scales=scales, in_=grouped.rearrange("p n t -> p (n t)"))

        def setup():
            nc.scalar.dma_start(out=gain[:], in_=whiten.rearrange("(g p t) -> p g t", p=P, t=PACK))
            nc.vector.memset(table_probe[:, 0, :], 0.0)
            nc.vector.memset(ones[:].bitcast(U32), TWO_BF16_ONES)
            quantize(ones_codes[:], ones_scales[:], ones[:])
            nc.vector.memset(v_scales_raw[:].bitcast(I32), 0)
            nc.vector.memset(c_scales[:].bitcast(I32), 0)
            make_identity(nc, identity[:])
            nc.scalar.activation(out=table_probe[:, 1, :], in_=table_probe[:, 0, :], func=ACT.Square)
            gain_columns = gain[:].rearrange("p g t -> p (g t)")
            nc.gpsimd.memset(one_half[:], 0.5)
            nc.scalar.activation(out=gain_size[:], in_=gain_columns, func=ACT.Abs)
            nc.scalar.activation(out=gain_sign[:], in_=gain_columns, func=ACT.Sign)
            nc.gpsimd.tensor_tensor(out=gain_root[:], in0=gain_size[:], in1=one_half[:], op=ALU.pow)

        def warm_up(passes):
            bank = take_bank("warm", [P, P])
            for n in range(passes):
                nc.tensor.matmul_mx(
                    out=bank[:],
                    lhsT=ones_codes[:].bitcast(FP8X4),
                    lhsT_scale=ones_scales[:],
                    rhs=ones_codes[:].bitcast(FP8X4),
                    rhs_scale=ones_scales[:],
                    start=True,
                    stop=True,
                )
            give_bank("warm")

        def load_frames(target, source, h, tiles):
            rows = source[h * W : (h + 1) * W, :].rearrange("(r i) k -> r i k", i=PACK)
            nc.sync.dma_start(out=target[:, h, tiles, :], in_=rows[:, tiles, :])

        def load_taps(g, c):
            rows = core_taps[c * W : (c + 1) * W, g * W : (g + 1) * W].rearrange("(p j) f -> p j f", j=PACK)
            nc.sync.dma_start(out=taps_raw[:, g, c], in_=rows)

        def load_v_words(groups):
            words = edge_taps_words[0][:, 2 * W * groups.start : 2 * W * groups.stop]
            target = v_words_raw[:, groups].rearrange("p g n -> p (g n)")
            nc.sync.dma_start(out=target.bitcast(I32), in_=words.bitcast(I32))

        def load_v_scales():
            plane = v_scales_raw[:].rearrange("p g n -> p (g n)").bitcast(I32)
            for q in range(P // QUADRANT):
                rows = edge_taps_scales[0][SCALE_ROWS * q : SCALE_ROWS * (q + 1), :]
                nc.sync.dma_start(out=plane[QUADRANT * q : QUADRANT * q + SCALE_ROWS, :], in_=rows.bitcast(I32))

        def load_c_words():
            nc.sync.dma_start(out=c_words[:].bitcast(I32), in_=combine_words.rearrange("g p n -> p g n").bitcast(I32))

        def load_c_scales():
            for q in range(P // QUADRANT):
                rows = combine_scales[:, SCALE_ROWS * q : SCALE_ROWS * (q + 1), :].rearrange("g r n -> r g n")
                target = c_scales[QUADRANT * q : QUADRANT * q + SCALE_ROWS]
                nc.sync.dma_start(out=target.bitcast(I32), in_=rows.bitcast(I32))

        def order_v_words(groups):
            nc.vector.tensor_copy(
                out=v_words[:, groups].rearrange("p g (t m b) -> p g t m b", t=PACK, b=2),
                in_=v_words_raw[:, groups].rearrange("p g (m t b) -> p g t m b", t=PACK, b=2),
            )

        def order_v_scales():
            nc.vector.tensor_copy(
                out=v_scales[:].rearrange("p g (t m) -> p g t m", t=PACK),
                in_=v_scales_raw[:].rearrange("p g (m t) -> p g t m", t=PACK),
            )

        def transpose(h, s, pair):
            bank = take_bank(("turned", h, s, pair), [P, 2, 2, P])
            samples = edge_raw[:, h] if s == 0 else core_raw[:, h, :, (s - 1) * W : s * W]
            words = samples.bitcast(F32)
            for i in range(2):
                for u in range(2):
                    nc.tensor.transpose(bank[:, i, u, :], words[:, 2 * pair + i, u : 2 * P : 2], identity[:])

        def unload(h, s, pair, engine):
            grouped = staging("samples_grouped", (h, s), [P, W, PACK], SAMPLE_BUFS)
            words = grouped[:].rearrange("p n t -> p (n t)").bitcast(F32)[:, pair * W : (pair + 1) * W]
            copy_on(
                engine,
                words.rearrange("p (i r u) -> p i r u", i=2, u=2),
                give_bank(("turned", h, s, pair))[:].rearrange("p i u r -> p i r u"),
            )

        def quantize_samples(h, s):
            quantize(sample_codes[:, h, s], sample_scales[:, h, s], staged["samples_grouped", (h, s)][:])

        def group_taps(g, c, columns, engine):
            grouped = staging("taps_grouped", (g, c), [P, W, PACK], TAPS_BUFS)
            tiles = slice(columns.start // P, columns.stop // P)
            copy_on(
                engine,
                grouped[:].rearrange("p (t a b) j -> p t a j b", t=PACK, b=2)[:, tiles],
                taps_raw[:, g, c].rearrange("p j (a b t) -> p t a j b", t=PACK, b=2)[:, tiles],
            )

        def quantize_taps(g, c):
            quantize(taps_codes[:, g, c], taps_scales[:, g, c], staged["taps_grouped", (g, c)][:])

        def filter_pass(h, g, t, s):
            if s == 0:
                take_bank(("y", h, g, t), [P, W])
                codes = v_words[:, g, 2 * P * t : 2 * P * (t + 1)].bitcast(FP4X4)
                scales = v_scales[:, g, P * t : P * (t + 1)]
            else:
                codes = taps_codes[:, g, s - 1, P * t : P * (t + 1)].bitcast(FP8X4)
                scales = taps_scales[:, g, s - 1, P * t : P * (t + 1)]
            nc.tensor.matmul_mx(
                out=banks["y", h, g, t][1][:],
                lhsT=codes,
                lhsT_scale=scales,
                rhs=sample_codes[:, h, s].bitcast(FP8X4),
                rhs_scale=sample_scales[:, h, s],
                start=(s == 0),
                stop=(s == CHUNKS - 1),
            )

        def chunk_passes(h, g, s, tiles=range(PACK)):
            for t in tiles:
                filter_pass(h, g, t, s)

        def filter_tile(h, g, t):
            for s in range(CHUNKS):
                filter_pass(h, g, t, s)

        def square(h, g, *tiles):
            squares = staging("squares", (h, g), [P, PACK, W], SQUARE_BUFS)
            for t in tiles:
                column = PACK * g + t
                nc.scalar.activation(
                    out=squares[:, t, :],
                    in_=give_bank(("y", h, g, t))[:],
                    func=ACT.Square,
                    scale=gain_root[:, column : column + 1],
                )

        def apply_sign(h, g):
            for t in range(PACK):
                column = PACK * g + t
                rows = staged["squares", (h, g)][:, t, :]
                nc.vector.tensor_scalar(
                    out=rows, in0=rows, scalar1=gain_sign[:, column : column + 1], scalar2=None, op0=ALU.mult
                )

        def group_energy(h, g, frames, engine):
            grouped = staging("energy_grouped", (h, g), [P, W, PACK], ENERGY_BUFS)
            copy_on(
                engine,
                grouped[:, frames, :].rearrange("p (a b) t -> p a t b", b=4),
                staged["squares", (h, g)][:, :, frames].rearrange("p t (a b) -> p a t b", b=4),
            )

        def quantize_energy(h, g, frames):
            grouped = staged["energy_grouped", (h, g)]
            quantize(energy_codes[:, h, g, frames], energy_scales[:, h, g, frames], grouped[:, frames, :])

        def band_pass(h, i, g):
            if g == 0:
                take_bank(("z", h, i), [P, BANDS])
            nc.tensor.matmul_mx(
                out=banks["z", h, i][1][:],
                lhsT=energy_codes[:, h, g, P * i : P * (i + 1)].bitcast(FP8X4),
                lhsT_scale=energy_scales[:, h, g, P * i : P * (i + 1)],
                rhs=c_words[:, g].bitcast(FP4X4),
                rhs_scale=c_scales[:, g],
                start=(g == 0),
                stop=(g == GROUPS - 1),
            )

        def band_passes(*steps):
            for h, i, g in steps:
                band_pass(h, i, g)

        def finish(h, i, bands=ALL):
            bank = give_bank(("z", h, i)) if bands.stop == BANDS else banks["z", h, i][1]
            nc.vector.tensor_tensor(
                out=result[:, h, i, bands], in0=bank[:, bands], in1=level_rows[:, bands], op=ALU.subtract
            )
            rows = out[h * W : (h + 1) * W, :].rearrange("(r i) b -> r i b", i=PACK)
            nc.sync.dma_start(out=rows[:, i, bands], in_=result[:, h, i, bands])

        setup()

        first_pair, second_pair, all_tiles = slice(0, 2), slice(2, PACK), slice(0, PACK)
        first_group, later_groups = slice(0, 1), slice(1, GROUPS)
        load_v_words(first_group)
        load_frames(edge_raw, edge, 0, first_pair)
        load_frames(edge_raw, edge, 0, second_pair)
        load_frames(core_raw, core, 0, first_pair)
        load_v_scales()
        load_frames(core_raw, core, 0, second_pair)
        load_frames(edge_raw, edge, 1, all_tiles)
        load_taps(0, 0)
        load_frames(core_raw, core, 1, first_pair)
        load_v_words(later_groups)
        load_taps(0, 1)
        load_frames(core_raw, core, 1, second_pair)
        load_taps(1, 0)
        load_taps(1, 1)
        load_taps(2, 0)
        load_taps(2, 1)
        load_c_scales()
        load_c_words()
        nc.sync.dma_start(out=level_rows[:], in_=level.partition_broadcast(P))


        warm_up(WARM_PASSES_AT_START)
        transpose(0, 0, 0)
        unload(0, 0, 0, "scalar")
        transpose(0, 0, 1)
        unload(0, 0, 1, "scalar")
        transpose(0, 1, 0)
        unload(0, 1, 0, "scalar")
        warm_up(WARM_PASSES_BETWEEN_LOADS)
        order_v_words(first_group)
        quantize_samples(0, 0)
        order_v_scales()
        transpose(0, 2, 0)
        unload(0, 2, 0, "scalar")
        transpose(0, 2, 1)
        unload(0, 2, 1, "scalar")
        transpose(0, 1, 1)
        unload(0, 1, 1, "scalar")
        quantize_samples(0, 2)
        transpose(1, 0, 0)
        transpose(1, 0, 1)

        group_taps(0, 0, FIRST, "scalar")
        group_taps(0, 0, SECOND, "vector")
        quantize_samples(0, 1)
        chunk_passes(0, 0, 0)
        unload(1, 0, 0, "scalar")
        unload(1, 0, 1, "scalar")
        transpose(1, 1, 0)
        transpose(1, 2, 0)
        quantize_taps(0, 0)
        order_v_words(later_groups)
        unload(1, 1, 0, "scalar")
        unload(1, 2, 0, "scalar")
        group_taps(0, 1, SECOND, "scalar")
        group_taps(0, 1, FIRST, "vector")
        quantize_samples(1, 0)
        chunk_passes(0, 0, 1)
        transpose(1, 1, 1)
        transpose(1, 2, 1)
        quantize_taps(0, 1)
        unload(1, 1, 1, "scalar")
        unload(1, 2, 1, "scalar")

        chunk_passes(1, 0, 0, tiles=(0, 1))
        chunk_passes(0, 0, 2)
        group_taps(1, 0, FIRST, "vector")
        quantize_samples(1, 1)
        quantize_samples(1, 2)
        group_taps(1, 0, SECOND, "scalar")
        group_taps(1, 1, FIRST, "vector")
        group_taps(1, 1, SECOND, "scalar")
        quantize_taps(1, 0)
        quantize_taps(1, 1)
        square(0, 0, 0, 1)
        chunk_passes(1, 0, 0, tiles=(2, 3))
        chunk_passes(1, 0, 1)
        chunk_passes(1, 0, 2)
        square(0, 0, 2, 3)

        group_taps(2, 0, ALL, "vector")
        group_taps(2, 1, ALL, "vector")
        filter_tile(0, 1, 0)
        square(1, 0, 0, 1)
        filter_tile(0, 1, 1)
        square(1, 0, 2, 3)
        filter_tile(1, 1, 0)
        quantize_taps(2, 0)
        quantize_taps(2, 1)
        apply_sign(0, 0)
        apply_sign(1, 0)
        filter_tile(0, 1, 2)
        square(0, 1, 0, 1)
        filter_tile(0, 1, 3)
        square(1, 1, 0)
        square(0, 1, 2)
        group_energy(0, 0, ALL, "vector")
        group_energy(1, 0, ALL, "vector")

        filter_tile(0, 2, 0)
        square(0, 1, 3)
        filter_tile(0, 2, 1)
        square(0, 2, 0)
        filter_tile(0, 2, 2)
        square(0, 2, 1)
        filter_tile(0, 2, 3)
        square(0, 2, 2)
        quantize_energy(0, 0, ALL)
        apply_sign(0, 1)
        quantize_energy(1, 0, ALL)
        filter_tile(1, 1, 1)
        square(0, 2, 3)
        apply_sign(0, 2)
        filter_tile(1, 1, 2)
        square(1, 1, 1)
        group_energy(0, 1, ALL, "vector")
        filter_tile(1, 1, 3)
        square(1, 1, 2)
        group_energy(0, 2, FIRST, "vector")
        filter_tile(1, 2, 0)
        square(1, 1, 3)
        group_energy(0, 2, SECOND, "scalar")
        apply_sign(1, 1)
        filter_tile(1, 2, 1)
        square(1, 2, 0)
        quantize_energy(0, 1, ALL)
        group_energy(1, 1, FIRST, "vector")
        filter_tile(1, 2, 2)
        square(1, 2, 1)
        filter_tile(1, 2, 3)
        square(1, 2, 2, 3)
        quantize_energy(0, 2, SECOND)
        quantize_energy(0, 2, FIRST)
        quantize_energy(1, 1, FIRST)
        apply_sign(1, 2)
        group_energy(1, 1, SECOND, "scalar")
        group_energy(1, 2, FIRST, "scalar")
        group_energy(1, 2, SECOND, "scalar")

        band_passes((0, 0, 0), (0, 0, 1), (0, 1, 0), (0, 1, 1), (0, 2, 0), (0, 0, 2))
        finish(0, 0)
        band_pass(0, 1, 2)
        quantize_energy(1, 1, SECOND)
        finish(0, 1)
        band_passes((0, 2, 1), (0, 2, 2))
        finish(0, 2)
        band_passes((1, 0, 0), (0, 3, 0), (0, 3, 1), (0, 3, 2))
        quantize_energy(1, 2, FIRST)
        finish(0, 3)
        band_passes((1, 0, 1), (1, 1, 0), (1, 1, 1), (1, 0, 2))
        quantize_energy(1, 2, SECOND)
        finish(1, 0)
        band_pass(1, 1, 2)
        finish(1, 1)
        band_passes((1, 2, 0), (1, 2, 1), (1, 2, 2))
        finish(1, 2)
        band_passes((1, 3, 0), (1, 3, 1), (1, 3, 2))
        finish(1, 3, FIRST)
        finish(1, 3, SECOND)
